import numpy as np, ml_dtypes
CORES = [10,34,74,98]
N = 4
import mx_ref
BF = ml_dtypes.bfloat16
def gentries(a):
    return np.ascontiguousarray(a.reshape(8, 16, -1).transpose(0, 2, 1)).reshape(8, -1)
def gtable(e):
    e = np.asarray(e); return np.ascontiguousarray(e.reshape(8, -1, 16).transpose(0, 2, 1)).reshape(128, -1).astype(np.int32)
def gcols(t, e):
    v = np.concatenate([t.reshape(8, 16, -1, 4), np.zeros((8, 16, 1, 4), BF)], axis=2)
    return np.ascontiguousarray(np.stack([v[g][:, e[g]] for g in range(8)])).reshape(128, -1)
def tile(rs):
    return np.stack(rs, axis=2).reshape(128, -1).astype(BF)
def pick(q, e):
    c = np.concatenate([q[0].reshape(128, -1, 4), np.zeros((128, 1, 4), np.uint8)], axis=1); s = np.concatenate([q[1], np.ones((16, 1), np.uint8)], axis=1)
    return (np.ascontiguousarray(c[:, e].reshape(128, -1)), np.ascontiguousarray(s[:, e]))
def join(*qs):
    return (np.concatenate([q[0] for q in qs], axis=1), np.concatenate([q[1] for q in qs], axis=1))
def put(q, e, v):
    c, s = q[0].reshape(128, -1, 4).copy(), q[1].copy(); c[:, e] = v[0].reshape(128, -1, 4); s[:, e] = v[1]
    return (c.reshape(128, -1), s)
def pk(c, s):
    return (np.ascontiguousarray(c), mx_ref.live(s))
def emit(q):
    return q[0], q[1]
def packed(v, rng):
    q = [mx_ref.quantize(np.ascontiguousarray(v[r])) for r in range(N)]
    return np.stack([a for a, b in q]), np.stack([mx_ref.plane(b, rng) for a, b in q])
def values_of_codes():
    e, c = np.zeros((128, 128, 4), np.float32), np.zeros((128, 2, 4), np.uint8)
    e[np.arange(128), np.arange(128), 0] = 1
    c[:127, :, 0] = np.arange(256).reshape(2, 128).T[:127]
    return mx_ref.matmul(mx_ref.quantize(e.reshape(128, 512).astype(BF)), (c.reshape(128, 8), np.full((16, 2), 127, np.uint8))).T.reshape(-1).astype(np.float64)
CODE_VALUE, SCALE_VALUE = values_of_codes(), 2.0 ** (np.arange(256) - 127.0)
def decode(q):
    return (CODE_VALUE[q[0]].reshape(16, 8, -1, 4) * SCALE_VALUE[q[1]][:, None, :, None] + 0.0).reshape(128, -1).astype(np.float32)
def f(rng, *shape):
    return mx_ref.flush((rng.standard_normal(shape, dtype=np.float32) * np.exp2(rng.integers(-2, 3, shape[:-1] + (1,)))).astype(BF))
def wide(rng, *shape, cols=0):
    v = rng.standard_normal(shape, dtype=np.float32) * np.exp2(rng.integers(-12, 13, shape)).astype(np.float32)
    if cols: v *= np.repeat(np.exp2(rng.integers(-cols, cols + 1, shape[:-2] + (1, shape[-1] // 4))) * (rng.random(shape[:-2] + (1, shape[-1] // 4)) > 0.0625), 4, axis=-1).astype(np.float32)
    return mx_ref.flush(v.astype(BF))
C, L, S, R = 384, 32, 24, 3
G = np.arange(8)[:, None]
def big(v):
    v = v.astype(np.float32)
    v[np.abs(v) < np.float32(2.0 ** -16)] = 0
    return v.astype(BF)
def numbers_of(rng):
    u = np.array(f(rng, N, 128, 512)).reshape(N, 8, 16, 128, 4)
    for g in range(8):
        u[:, :g, :, 16 * g] = 0
        u[:, g + 1:, :, 16 * g] = 0
    return {"x": big(f(rng, N, 128, 4 * C)), "u": u.reshape(N, 128, 512), "v": np.array(f(rng, N, 128, 512))}
def layers(rng):
    return big(f(rng, N, 128, 2048)).reshape(N, 8, 16, 4, 8, 16, 4)
def weights(rng, w):
    c, p = packed(np.ascontiguousarray(w).reshape(N, 128, 2048), rng)
    return {"wc": c, "ws": p}
def routes(rng):
    return np.argsort(rng.random((N, 8, 2 * C)), axis=2) % C
def walks(rng):
    return rng.integers(0, C, (N, 8, C))
def ways(e, w):
    return {"rt": np.stack([gtable(a) for a in e]), "ft": np.stack([gtable(a) for a in w])}
def setup_inputs(rng):
    return {**numbers_of(rng), **weights(rng, layers(rng)), **ways(routes(rng), walks(rng))}
def setup_inputs_ties(rng):
    d = numbers_of(rng)
    e = rng.permutation(N)
    x = d["x"].reshape(N, 8, 16, C, 4)
    a = x[0][:, :8, :3].copy()
    a[:, :, 2] = 0
    for r in range(N):
        k = rng.permutation(C) % 3
        if r == e[0]: k = np.zeros(C, int)
        if r == e[1]: k = np.full(C, 2)
        x[r][:, :8] = a[:, :, k]
    u = d["u"].reshape(N, 8, 16, 128, 4)
    u[:, :, 8:, ::16] = 0
    w = layers(rng)
    w[:, :, :, :, :, :8] = 0
    return {"x": x.reshape(N, 128, 4 * C), "u": u.reshape(N, 128, 512), "v": d["v"], **weights(rng, w), **ways(routes(rng), walks(rng))}
def setup_inputs_near(rng):
    d = numbers_of(rng)
    x = np.zeros((N, 8, 16, C, 4), np.float32)
    u = d["u"].reshape(N, 128, 128, 4)
    u[:, :, ::16] = 0
    o, c = rng.permutation(N) % 4, rng.permutation(8) % 2 * 2.0 - 1.0
    e = np.zeros((N, 8, 2 * C), int)
    for r in range(N):
        i = (np.arange(C) + rng.integers(0, C, (8, 1))) % C
        e[r, :, :C] = np.argsort(i, axis=1)
        e[r, :, C:] = np.argsort(rng.random((8, C)), axis=1)
        size = 1.0 if o[r] < 2 else 2.0 ** -4
        z = (((i // 2)[:, :, None] >> np.arange(8)) & 1) * np.exp2(np.arange(8) - 23.0) * size
        x[r, :, 0, :, 0] = c[:, None] * (1 - r % 2 * 2) if o[r] < 2 else (8 + i % 2) * 2.0 ** -30
        x[r, :, 8] = z[:, :, :4]
        x[r, :, 9] = z[:, :, 4:]
        x[r, :, 10:] = rng.integers(4, 8, (8, 6, C, 4)) * 2.0 ** -20 * size
        k = 1.0 if o[r] == 0 else 2.0 ** -30
        for h in range(0, 128, 16):
            u[r, h, h, 0] = k
            u[r, h + 8:h + 10, h] = k
    w = layers(rng)
    w[:, :, :10] = 0
    w[:, :, :, :, :, :10] = 0
    return {"x": x.reshape(N, 128, 4 * C).astype(BF), "u": u.reshape(N, 128, 512), "v": d["v"], **weights(rng, w), **ways(e, walks(rng))}
def setup_inputs_huge(rng):
    d = numbers_of(rng)
    c = np.stack([np.where(rng.permutation(C) % 2 == 0, -1.0, 0.25) for r in range(N)])
    c[rng.permutation(N) < N // 2] = -1
    x = 2.0 ** 30 * (0.8 + 0.2 * rng.random((N, 128, C, 4))) * c[:, None, :, None]
    s = np.stack([rng.permutation(8) % 2 * 2.0 - 1.0 for r in range(N)])
    a = 2.0 ** 30 * (1 - 0.1 * rng.random((N, 8, 16, 4))) * s[:, :, None, None]
    u = d["u"].reshape(N, 8, 16, 128, 4)
    for g in range(8): u[:, g, :, 16 * g] = a[:, g].astype(np.float32).astype(BF)
    w = np.zeros((N, 128, 4, 128, 4), np.float32)
    i = np.arange(128)
    for b in range(4): w[:, i, b, i, b] = -4
    return {"x": x.astype(np.float32).reshape(N, 128, 4 * C).astype(BF), "u": u.reshape(N, 128, 512), "v": d["v"], **weights(rng, w.astype(BF)), **ways(routes(rng), walks(rng))}
def setup_inputs_routes(rng):
    d = numbers_of(rng)
    x, u = d["x"].reshape(N, 8, 16, C, 4), d["u"].astype(np.float32).reshape(N, 8, 16, 128, 4)
    e, w = routes(rng), walks(rng)
    n = np.arange(C)
    for r in range(N):
        for g, k in enumerate(rng.permutation(8)):
            p = rng.permutation(C)
            if k == 0: e[r, g], w[r, g] = np.concatenate([p, p]), n
            if k == 1: e[r, g], w[r, g] = np.repeat(p, 2), (n + 1) % C
            if k == 2: e[r, g], w[r, g] = np.concatenate([p, p[::-1]]), (n - 1) % C
            if k == 3: e[r, g], w[r, g] = np.tile(p.reshape(L, S // 2), 2).reshape(-1), p[0]
            if k == 4:
                a = np.zeros((L, S), int)
                a[:, 0] = np.tile(p[:L // 2], 2)
                a[:, 1:] = rng.permutation(np.tile(p[L // 2:], 2)).reshape(L, S - 1)
                e[r, g], w[r, g] = a.reshape(-1), n ^ 1
            if k == 5:
                w[r, g] = e[r, g, 1]
                x[r, g, :, e[r, g, 0]] = (16 * np.sign(u[r, g, :, 16 * g])).astype(BF)
    return {"x": x.reshape(N, 128, 4 * C), "u": d["u"], "v": d["v"], **weights(rng, layers(rng)), **ways(e, w)}
def setup_inputs_spread(rng):
    d = setup_inputs(rng)
    d["x"] = big(wide(rng, N, 128, 4 * C, cols=6))
    return d
def check_inputs(d):
    b = []
    for k in ("x", "u", "v"):
        a = np.abs(d[k].astype(np.float32))
        if not (np.isfinite(a).all() and ((a == 0) | (a >= 2.0 ** -30) & (a <= 2.0 ** 30)).all()): b.append("a value of " + k)
    a = d["u"].astype(np.float32).reshape(N, 8, 16, 128, 4)
    for g in range(8):
        if (np.delete(a[:, :, :, 16 * g], g, axis=1) != 0).any(): b.append("u: a column that scores a group isn't zero outside it")
    none, least, most = [emit(mx_ref.quantize(np.full((128, 16), k, np.float32).astype(BF)))[1][0, 0] for k in (0.0, 2.0 ** -30, 2.0 ** 30)]
    for r in range(N):
        if ((d["wc"][r] == 0x7F) | (d["wc"][r] == 0xFF)).any(): b.append("wc: a code that is no number")
        s = mx_ref.live(d["ws"][r])
        if ((s != none) & ((s < least) | (s > most))).any(): b.append("ws: a scale out of range")
        if (np.sort(gentries(d["rt"][r]), axis=1) != np.arange(2 * C) // 2).any(): b.append("rt: a stop that isn't there exactly twice")
    if ((d["ft"] < 0) | (d["ft"] >= C)).any(): b.append("ft: a number that is no stop")
    return b
def reference(x, u, v, wc, ws, rt, ft):
    qu = [mx_ref.quantize(u[r]) for r in range(N)]
    lay = [pk(wc[r], ws[r]) for r in range(N)]
    way = [gentries(rt[r]) for r in range(N)]
    foot = [gentries(ft[r]) for r in range(N)]
    at = [np.argsort(way[r], axis=1, kind="stable").reshape(8, C, 2) for r in range(N)]
    now = [x[r] for r in range(N)]
    last = [None] * N
    for t in range(R):
        own, score, sent = [], [], []
        for r in range(N):
            q = mx_ref.quantize(now[r])
            s = mx_ref.matmul(qu[r], q)[::16] + np.float32(0.0)
            z = s[G, way[r]].reshape(8, L, S)
            e = np.take_along_axis(way[r].reshape(8, L, S), np.argmax(z, axis=2)[:, :, None], axis=2)[:, :, 0]
            own.append(decode(q))
            score.append(z)
            sent.append(mx_ref.quantize(gcols(now[r], e)))
        for r in range(N):
            guests = sent[(r - 1 - t) % N]
            z = mx_ref.matmul(qu[r], guests)[::16] + np.float32(0.0)
            c = np.concatenate([z[:, :, None], score[r][:, :, :S - 1]], axis=2)
            src = np.concatenate([np.tile(C + np.arange(L), (8, 1))[:, :, None], way[r].reshape(8, L, S)[:, :, :S - 1]], axis=2)
            m = np.maximum.accumulate(c, axis=2)
            above = np.zeros((8, L, S), bool)
            above[:, :, 1:] = c[:, :, 1:] > m[:, :, :-1]
            k = np.maximum.accumulate(np.where(above, np.arange(S), 0), axis=2)
            a, val = np.take_along_axis(src, k, axis=2).reshape(8, -1), m.reshape(8, -1)
            p0, p1 = at[r][:, :, 0], at[r][:, :, 1]
            p = np.where(val[G, p1] > val[G, p0], p1, p0)
            a, val = a[G, p], val[G, p]
            a = a[G, np.where(val[G, foot[r]] > val, foot[r], np.arange(C))]
            both = np.concatenate([own[r], decode(guests)], axis=1).astype(BF)
            q = mx_ref.quantize(((own[r] + gcols(both, a).astype(np.float32)) * np.float32(0.5)).astype(BF))
            now[r] = tile([own[r][:, b::4] + np.maximum(mx_ref.matmul(pick(lay[r], np.arange(128 * b, 128 * b + 128)), q), np.float32(0.0)) * np.float32(0.03125) for b in range(4)])
            last[r] = a
    y, oa = np.zeros((N, 128, C), np.float32), np.zeros((N, 8, C), np.float32)
    oc, osc = np.zeros((N, 128, 4 * C), np.uint8), np.zeros((N, 16, C), np.uint8)
    for r in range(N):
        q = mx_ref.quantize(now[r])
        y[r] = mx_ref.matmul(mx_ref.quantize(v[r]), q)
        oa[r] = last[r]
        oc[r], osc[r] = emit(q)
    return {"y": y, "oa": oa, "oc": oc, "osc": osc}

@@ -1,0 +1,538 @@
+from concourse.bass import DstId, RemoteDMATransfer
+from concourse.mybir import dt, AluOpType, AxisListType, ActivationFunctionType
+
+C, L, S, R = 384, 32, 24, 3
+H = C // 2
+B = C + L
+BIG = 1e29
+CODE = "float8_e4m3fn_x4"
+IN_ORDER = True
+EARLY = 1
+
+
+def _sb(n, d="float32"):
+    return ("sbuf", [128, n], d)
+
+
+SCRATCH = {
+    "xt": _sb(4 * C, "bfloat16"), "yt": _sb(4 * C, "bfloat16"), "et": _sb(512, "bfloat16"),
+    "ut": _sb(512, "bfloat16"), "vt": _sb(512, "bfloat16"), "bh": _sb(4 * B, "bfloat16"), "pb": _sb(2 * C, "bfloat16"),
+    "fh": _sb(2 * C, "bfloat16"), "jb": _sb(12),
+    "ones": _sb(516, "bfloat16"), "ida": _sb(516, "bfloat16"), "idb": _sb(516, "bfloat16"), "idh": _sb(1024, "bfloat16"),
+    "cap16": _sb(C, "bfloat16"),
+    "qu": _sb(128, CODE), "su": _sb(128, "uint8"), "qp": _sb(256, CODE), "sp": _sb(256, "uint8"),
+    "qv": _sb(128, CODE), "sv": _sb(128, "uint8"), "qw": _sb(512, CODE), "sw": _sb(512, "uint8"),
+    "qi": _sb(768, CODE), "si": _sb(768, "uint8"), "qy": _sb(C, CODE), "sy": _sb(C, "uint8"),
+    "rti": _sb(48, "int32"), "fti": _sb(24, "int32"), "rowi": _sb(768, "int32"),
+    "ci": _sb(8, "int32"), "cf": _sb(16), "i1": _sb(144), "i2": _sb(96, "int32"), "i3": _sb(96, "int32"),
+    "i4": _sb(96, "int32"), "iu": _sb(16, "int32"), "fld": _sb(576, "int32"), "eq": _sb(32), "capg": _sb(32),
+    "capr": _sb(48), "cap4": _sb(96), "jrow": _sb(B), "tab": _sb(576), "key": _sb(96), "sums": _sb(12),
+    "uoff": _sb(16, "uint16"), "koff": _sb(96, "uint16"), "zoff": _sb(48, "uint16"), "roff": _sb(48, "uint16"),
+    "foff": _sb(24, "uint16"), "coff": _sb(48, "uint16"), "loff": _sb(96, "uint16"), "eoff": _sb(8, "uint16"),
+    "aoff": _sb(24, "uint16"), "goff": _sb(96, "uint16"), "gwin": _sb(2 * L), "vv": _sb(96), "aa": _sb(96),
+    "way": _sb(48), "wrow": _sb(768), "swin": _sb(768), "b0": _sb(1536), "b1": _sb(1536), "b2": _sb(1536), "b3": _sb(1536),
+    "rin": _sb(1536), "rr": _sb(4 * C), "mm": _sb(49), "ss": _sb(49), "ab": _sb(96), "na": _sb(96), "ta": _sb(96),
+    "md": _sb(96), "sd": _sb(96), "gm": _sb(32), "gg": _sb(2), "tp": _sb(96), "m4": _sb(97), "s4": _sb(96),
+    "f1": _sb(96), "f2": _sb(96), "yo": _sb(C), "oar": _sb(C),
+}
+for _t in range(R + 1):
+    SCRATCH["qt%d" % _t] = _sb(B, CODE)
+    SCRATCH["st%d" % _t] = _sb(512, "uint8")
+for _t in range(R):
+    SCRATCH["qe%d" % _t] = _sb(128, CODE)
+    SCRATCH["se%d" % _t] = _sb(128, "uint8")
+for _b in range(8):
+    SCRATCH["p%d" % _b] = ("psum", [128, 512], "float32")
+
+POOL = {"V": 50, "A": 30, "P": 20, "G": 10}
+SEMAPHORES = (["sent"] + ["arr%d" % t for t in range(R)] + ["d%d" % i for i in range(30)]
+              + ["%s%d" % (e.lower(), i) for e in POOL for i in range(1 if IN_ORDER else POOL[e])])
+
+
+def _mask(v):
+    m = 0
+    for j in range(v[1], v[2], v[3]):
+        m |= 1 << j
+    return m
+
+
+def _emit(g, T, ops):
+    queue = {"V": g.vector, "A": g.scalar, "P": g.tensor, "G": g, "Y": g.sync}
+    seen = {}
+    for n, o in enumerate(ops):
+        deps = set()
+        for v, wr in [(v, False) for v in o["r"]] + [(v, True) for v in o["w"]]:
+            m = _mask(v)
+            psum = SCRATCH[v[0]][0] == "psum"
+            for e in seen.setdefault(v[0], []):
+                if (e[1] & m and (wr or e[2])) or (psum and ops[e[0]]["q"] != o["q"]):
+                    deps.add(e[0])
+        for v, wr in [(v, False) for v in o["r"]] + [(v, True) for v in o["w"]]:
+            m = _mask(v)
+            lst = seen[v[0]]
+            if wr:
+                for e in lst:
+                    e[1] &= ~m
+                lst[:] = [e for e in lst if e[1]]
+            lst.append([n, m, wr])
+        deps.discard(n)
+        o["deps"] = deps
+    known = {q: set() for q in queue}
+    earlier = {q: [] for q in queue}
+    for n, o in enumerate(ops):
+        o["waits"] = []
+        if o["q"] is None:
+            o["known"] = set()
+            continue
+        k = known[o["q"]]
+        for d in sorted(o["deps"], reverse=True):
+            if d not in k:
+                o["waits"].append(d)
+                ops[d]["needed"] = True
+                k.add(d)
+                k |= ops[d]["known"]
+        o["known"] = set(k)
+        if IN_ORDER and not o["dma"]:
+            o["known"] |= set(earlier[o["q"]])
+            earlier[o["q"]].append(n)
+    count, turn, dmas, last = {}, {q: 0 for q in queue}, 0, []
+    for o in ops:
+        if o["q"] is None:
+            continue
+        q = queue[o["q"]]
+        for d in o["waits"]:
+            q.wait_ge(T.sem[ops[d]["sig"][0]], ops[d]["sig"][1])
+        ins = o["f"]()
+        if o["dma"]:
+            o["sig"] = ("d%d" % dmas, 16)
+            dmas += 1
+            ins.then_inc(T.sem[o["sig"][0]], 16)
+            if not o.get("needed"):
+                last.append((q, o["sig"]))
+        elif o.get("needed"):
+            name = "%s%d" % (o["q"].lower(), 0 if IN_ORDER else turn[o["q"]] % POOL[o["q"]])
+            turn[o["q"]] += 1
+            count[name] = count.get(name, 0) + 1
+            o["sig"] = (name, count[name])
+            ins.then_inc(T.sem[name], 1)
+    for q, sig in last:
+        q.wait_ge(T.sem[sig[0]], sig[1])
+
+
+def rank_program(g, core, T, topo):
+    rank = T.rank_of(core)
+    if rank is None:
+        return
+    N = len(T.cores)
+    A, F = AluOpType, ActivationFunctionType
+    ops = []
+
+    def v(name, a=0, b=None, s=1):
+        return (name, a, SCRATCH[name][1][1] if b is None else b, s)
+
+    def ap(x):
+        if len(x) == 2:
+            return ap(x[0]).indirect(ap(x[1]))
+        return T[x[0]][:, x[1]:x[2]:x[3]] if x[3] != 1 else T[x[0]][:, x[1]:x[2]]
+
+    def rd(*xs):
+        out = []
+        for x in xs:
+            if isinstance(x, tuple):
+                out += list(x) if len(x) == 2 else [x]
+        return out
+
+    def add(q, f, r, w, dma=False):
+        ops.append({"q": q, "f": f, "r": r, "w": w, "dma": dma})
+
+    def sc(x):
+        return ap(x) if isinstance(x, tuple) else x
+
+    def copy(o, i):
+        add("V", lambda: g.vector.tensor_copy(ap(o), ap(i)), rd(i), [o])
+
+    def tt(o, a, b, op):
+        add("V", lambda: g.vector.tensor_tensor(ap(o), ap(a), ap(b), op), rd(a, b), [o])
+
+    def ts(o, a, s1, op0, s2=None, op1=None):
+        if op1 is None:
+            add("V", lambda: g.vector.tensor_scalar(ap(o), ap(a), sc(s1), None, op0), rd(a, s1), [o])
+        else:
+            add("V", lambda: g.vector.tensor_scalar(ap(o), ap(a), sc(s1), sc(s2), op0, op1), rd(a, s1, s2), [o])
+
+    def scan(o, a, b, init, op0, op1):
+        add("V", lambda: g.vector.tensor_tensor_scan(ap(o), ap(a), ap(b), init, op0, op1), rd(a, b), [o])
+
+    def fill(o, c):
+        add("V", lambda: g.vector.memset(ap(o), c), [], [o])
+
+    def turn(o, i):
+        add("V", lambda: g.vector.transpose(ap(o), ap(i)), [i], [o])
+
+    def rmax(o, i):
+        add("V", lambda: g.vector.tensor_reduce(ap(o), ap(i), AxisListType.X, A.max), [i], [o])
+
+    def act(o, i, func=F.Copy, scale=1.0, acc=None, bias=None):
+        if bias is not None:
+            add("A", lambda: g.scalar.activation(ap(o), ap(i), func, bias=ap(bias)), rd(i, bias), [o])
+        elif SCRATCH[o[0]][2] == "uint8":
+            add("A", lambda: g.scalar.activation(ap(o), ap(i), func), rd(i), [o])
+        elif acc is None:
+            add("A", lambda: g.scalar.activation(ap(o), ap(i), func, scale=scale), rd(i), [o])
+        else:
+            add("A", lambda: g.scalar.activation(ap(o), ap(i), func, accum_out=ap(acc)), rd(i), [o, acc])
+
+    def const(o, c):
+        act(o, v("ones", 0, len(range(*o[1:]))), scale=c)
+
+    def quant(q, s, a, b, i):
+        add("V", lambda: g.vector.quantize_mx(ap(v(q, a, b)), ap(v(s, a, b)), ap(i)), [i], [v(q, a, b), v(s, a, b)])
+
+    def mx(bank, lq, ls, la, rq, rs, a, b):
+        x = [v(lq, la, la + 128), v(ls, la, la + 128), v(rq, a, b), v(rs, a, b)]
+        o = v("p%d" % bank, 0, b - a)
+        add("P", lambda: g.tensor.matmul_mx(ap(o), ap(x[0]), ap(x[1]), ap(x[2]), ap(x[3]), True, True), x, [o])
+
+    def iota(o, pattern, base=0, cm=0):
+        if SCRATCH[o[0]][2] == "int32":
+            add("G", lambda: g.iota(ap(o), pattern, base, cm), [], [o])
+        else:
+            add("G", lambda: g.iota(ap(o), pattern, base, cm, allow_small_or_imprecise_dtypes=True), [], [o])
+
+    def dma(q, out, in_, r, w):
+        eng = g.sync if q == "Y" else g.scalar
+        add(q, lambda: eng.dma_start(out, in_), r, w, True)
+
+    def col(j):
+        return v("cf", j, j + 1)
+
+    K, U, K24, K16, GID, U384, N384, C32, U32, N32 = 0, 1, 2, 3, 4, 6, 7, 8, 9, 10
+
+    fill(v("rowi"), 0)
+    dma("Y", T.rti[:], T.rt[:], [], [v("rti")])
+    dma("Y", T.ut[:], T.u[:], [], [v("ut")])
+    dma("Y", T.rowi[0:128:16, :], T.rt[:], [], [v("rowi")])
+    for c in range(2):
+        dma("Y", ap(v("xt", 4 * H * c, 4 * H * (c + 1))), T.x[:, 4 * H * c:4 * H * (c + 1)], [], [v("xt", 4 * H * c, 4 * H * (c + 1))])
+    iota(v("ci", 0, 1), [[0, 1]], 0, 1)
+    iota(v("i1", 0, 48), [[384, 2], [1, 24]])
+    iota(v("capg"), [[0, 2], [1, 16]])
+    iota(v("iu", 0, 8), [[32, 4], [-16, 2]], 16)
+    iota(v("i1", 48, 96), [[1, 16], [256, 3]])
+    iota(v("iu", 8, 16), [[16, 8]])
+    iota(v("i1", 96, 144), [[16, 48]])
+    iota(v("jb"), [[32, 12]])
+    fill(v("ones"), 1.0)
+    for name, base in (("ida", 2), ("idb", 3)):
+        add("G", lambda name=name, base=base: g.affine_select(T[name][:], T.ones[:], [[-1, 516]], A.is_equal, 0.0, base, 4),
+            [v("ones")], [v(name)])
+    iota(v("jrow"), [[1, B]])
+    ts(v("ci", 2, 3), v("ci", 0, 1), 15, A.bitwise_and)
+    ts(v("ci", 3, 4), v("ci", 0, 1), 4, A.logical_shift_right, 1, A.bitwise_and)
+    const(v("tab", 0, H), 0.0)
+    const(v("tab", C, C + H), 0.0)
+    const(v("capr"), BIG)
+    const(v("mm", 0, 1), -BIG)
+    const(v("m4", 0, 1), -BIG)
+    const(v("ss", 0, 1), 0.0)
+    const(v("capr", S - 1, 48, S), -BIG)
+    copy(v("cf", 0, 2), v("ci", 2, 4))
+    ts(col(K24), col(K), 24.0, A.mult)
+    ts(v("eq"), v("capg"), col(K), A.is_equal)
+    ts(col(K16), col(K), 16.0, A.mult)
+    ts(v("i2", 0, 48), v("i1", 0, 48), col(K24), A.add)
+    ts(col(U384), col(U), float(C), A.mult)
+    ts(v("i3", 0, 48), v("i2", 0, 48), 15, A.bitwise_and)
+    ts(v("i4", 0, 48), v("i2", 0, 48), 4, A.logical_shift_right)
+    for m in range(12):
+        act(v("tab", H + 16 * m, H + 16 * m + 16), v("eq", 0, 16), scale=4.0 ** (3 * (m % 4) + m // 4))
+    ts(v("i3", 0, 48), v("i3", 0, 48), 48.0, A.mult)
+    ts(col(N384), col(U), -float(C), A.mult, float(C), A.add)
+    tt(v("i2", 0, 48), v("i3", 0, 48), v("i4", 0, 48), A.add)
+    copy(v("uoff"), v("iu"))
+    copy(v("koff", 0, 48), v("i2", 0, 48))
+    ts(v("koff", 48, 96), v("i1", 48, 96), col(K16), A.add)
+    ts(col(GID), col(K), float(C), A.add)
+    ts(col(GID + 1), col(K), float(C + 16), A.add)
+    ts(v("capg"), v("eq"), 2 * BIG, A.mult, -BIG, A.add)
+    ts(v("f2", 0, 48), v("i1", 96, 144), col(K), A.add)
+    ts(col(C32), col(U), 16.0, A.mult, col(K), A.add)
+    copy(v("roff"), v("rti"))
+    ts(v("jb"), v("jb"), col(C32), A.add, -2048.0, A.mult)
+    quant("qu", "su", 0, 128, v("ut"))
+
+    def pick(a):
+        o, off = v("qp", a, a + 128), v("uoff", a // 16, a // 16 + 8)
+        add("V", lambda: g.vector.tensor_copy(ap(o).bitcast(dt.uint32), T.qu[:, 0:128].bitcast(dt.uint32).indirect(ap(off))),
+            [v("qu"), off], [o])
+        act(v("sp", a, a + 128), (v("su"), off))
+
+    def counts(p):
+        act(v("b2", 768 * p, 768 * p + 768), (v("tab", H * (1 - p), H * (1 - p) + C), v("roff")))
+
+    def running(p):
+        x = v("b2", 768 * p, 768 * p + 768)
+        scan(v("rin", 768 * p, 768 * p + 768), x, x, 0.0, A.add, A.max)
+
+    copy(v("b0", 0, 768), (v("rowi"), v("koff", 0, 48)))
+    counts(0)
+    pick(0)
+    act(v("wrow"), (v("b0", 0, 768), v("koff", 48, 96)))
+    dma("Y", T.way[:], T.wrow[0:128:16, :], [v("wrow")], [v("way")])
+    dma("Y", T.fti[:], T.ft[:], [], [v("fti")])
+    dma("Y", T.qw[:].bitcast(dt.uint8), T.wc[:], [], [v("qw")])
+    dma("Y", T.sw[:], T.ws[:], [], [v("sw")])
+    dma("Y", T.vt[:], T.v[:], [], [v("vt")])
+
+    def scores(t, c):
+        mx(4 + 2 * c, "qu", "su", 0, "qt%d" % t, "st%d" % t, H * c, H * c + H)
+        mx(5 + 2 * c, "qp", "sp", 0, "qt%d" % t, "st%d" % t, H * c, H * c + H)
+        act(v("swin", H * c, H * c + H), v("p%d" % (4 + 2 * c), 0, H))
+        (act if c == 0 or t == 0 else copy)(v("swin", C + H * c, C + H * c + H), v("p%d" % (5 + 2 * c), 0, H))
+
+    for c in range(2):
+        quant("qt0", "st0", H * c, H * c + H, v("xt", 4 * H * c, 4 * H * (c + 1)))
+        scores(0, c)
+    turn(v("b1", 0, 768), v("b0", 0, 768))
+    ts(v("zoff", 0, 48, 2), v("b1", 0, 768, 32), col(U384), A.add)
+    ts(v("zoff", 1, 48, 2), v("b1", 16, 768, 32), col(N384), A.add)
+    running(0)
+
+    def places():
+        running(1)
+        const(v("cap16"), -1.0)
+        const(v("cap4"), BIG)
+        for b in range(2):
+            act(v("idh", 512 * b, 512 * b + 512), v("idb" if b else "ida", 0, 512), scale=0.5)
+        const(v("cap16", 0, C, 16), 2.0 ** 21)
+        const(v("cap4", 3, 96, 4), -BIG)
+        copy(v("i2"), v("rin", 15, 1536, 16))
+        ts(v("f1", 0, 48), v("rti"), 2048.0, A.mult)
+        for r in range(6):
+            ts(v("fld", 96 * r, 96 * r + 96), v("i2"), r, A.logical_shift_right, 0x041041, A.bitwise_and)
+        for h in range(2):
+            copy(v("b0", 288 * h, 288 * h + 288), v("fld", 288 * h, 288 * h + 288))
+            for r in range(3 * h, 3 * h + 3):
+                for p in range(2):
+                    j = 6 * (r % 2) + 3 * p + r // 2
+                    act(v("b1", 48 * j, 48 * j + 48), v("b0", 96 * r + 48 * p, 96 * r + 48 * p + 48), acc=v("sums", j, j + 1))
+        tt(v("key", 0, 48), v("f1", 0, 48), v("f2", 0, 48), A.add)
+        tt(v("f1", 48, 96), v("f1", 0, 48), v("f2", 0, 48), A.subtract)
+        copy(v("foff"), v("fti"))
+        ts(v("key", 48, 96), v("f1", 48, 96), 1023.0, A.add)
+        for b in range(2):
+            quant("qi", "si", 128 * b, 128 * b + 128, v("idb" if b % 2 else "ida", 2, 514))
+        copy(v("i3", 0, 12), v("sums"))
+        for f in range(4):
+            ts(v("i4", f, 48, 4), v("i3", 0, 12), 6 * f, A.logical_shift_right, 63, A.bitwise_and)
+        tt(v("i4", 0, 24), v("i4", 0, 24), v("i4", 24, 48), A.add)
+        for p in range(2):
+            for h in range(2):
+                ts(v("coff", 2 * p + h, 48, 4), v("i4", 24 * p + h, 24 * p + 24, 2), -1.0, A.mult, 48.0 * (p + 1), A.add)
+        for p in range(2):
+            act(v("b0", C * p, C * p + C), (v("key"), v("coff", 24 * p, 24 * p + 24)))
+        for b in range(2, 4):
+            quant("qi", "si", 128 * b, 128 * b + 128, v("idb" if b % 2 else "ida", 0, 512))
+        quant("qi", "si", 512, 768, v("idh"))
+        turn(v("b1", 0, C), v("b0", 0, C))
+        for d in range(2):
+            copy(v("md", d, 96, 2), v("mm", 0, 48))
+            copy(v("sd", d, 96, 2), v("ss", 0, 48))
+        turn(v("b1", C, 2 * C), v("b0", C, 2 * C))
+        for b in range(12):
+            act(v("b2", 64 * b, 64 * b + 64), v("b1", 64 * b, 64 * b + 64), F.Abs, bias=v("jb", b, b + 1))
+        for p in range(2):
+            scan(v("b3", C * p, C * p + C), v("cap16"), v("b2", C * p, C * p + C), 0.0, A.max, A.min)
+        pick(128)
+        unpack(0)
+        for h in range(2):
+            copy(v("i2", h, 24, 2), v("b3", 15 + 16 * h, 2 * C, 64))
+            ts(v("i2", 24 + h, 48, 2), v("b3", 47 + 16 * h, 2 * C, 64), -1.0, A.mult, 1023.0, A.add)
+        ts(v("i3", 0, 48), v("i2", 0, 48), 2731.0, A.mult)
+        for h in range(2):
+            ts(v("f1", h, 48, 2), v("i2", h, 48, 2), 32.0, A.mult, 16.0 * h, A.add)
+        ts(v("i4", 0, 48), v("i3", 0, 48), 16, A.logical_shift_right)
+        ts(v("i4", 48, 96), v("i3", 0, 48), 20, A.logical_shift_right)
+        ts(v("f2", 0, 48), v("i4", 0, 48), -767.0, A.mult)
+        ts(v("f2", 48, 96), v("i4", 48, 96), 752.0, A.mult)
+        tt(v("f1", 48, 96), v("f1", 0, 48), v("f2", 0, 48), A.add)
+        for p in range(2):
+            tt(v("b0", p, C, 16), v("f1", 48 + 24 * p, 72 + 24 * p), v("f2", 48 + 24 * p, 72 + 24 * p), A.add)
+        turn(v("b1", 0, C), v("b0", 0, C))
+        act(v("wrow", 0, C), (v("b1", 0, C), v("foff")))
+        for p in range(2):
+            for h in range(2):
+                copy(v("loff", 2 * p + h, 96, 8), v("b0", 16 * h + p, C, 32))
+
+    def walked():
+        turn(v("b3", 0, C), v("wrow", 0, C))
+        for p in range(2):
+            for h in range(2):
+                copy(v("loff", 4 + 2 * p + h, 96, 8), v("b3", 16 * h + p, C, 32))
+
+    def unpack(t):
+        for b in range(4):
+            mx(b, "qi", "si", 128 * b, "qt%d" % t, "st%d" % t, 0, C)
+            act(v("bh", B * b, B * b + C), v("p%d" % b, 0, C), scale=0.5)
+            if b < 2:
+                act(v("fh", C * b, C * b + C), v("p%d" % b, 0, C), scale=0.5)
+        for b in range(2):
+            mx(6 + b, "qi", "si", 512 + 128 * b, "qt%d" % t, "st%d" % t, 0, C)
+
+    for t in range(R):
+        qt, st, qe, se = "qt%d" % t, "st%d" % t, "qe%d" % t, "se%d" % t
+        for j in range(2):
+            act(v("b0", 256 * j, 256 * j + 256), (v("swin"), v("zoff", 16 * j, 16 * j + 16)))
+        copy(v("b0", 512, 768), (v("swin"), v("zoff", 32, 48)))
+        for j in (2, 0, 1):
+            turn(v("b1", 256 * j, 256 * j + 256), v("b0", 256 * j, 256 * j + 256))
+        z = v("b1", 0, 768, 16)
+        if t == 0:
+            const(v("et", 4 * L, 512), 0.0)
+            counts(1)
+        scan(v("mm", 1, 49), z, v("capr"), -BIG, A.max, A.min)
+        tt(v("ab", 0, 48), z, v("mm", 0, 48), A.is_gt)
+        tt(v("na", 0, 48), z, v("mm", 0, 48), A.is_le)
+        tt(v("ta", 0, 48), v("ab", 0, 48), v("way"), A.mult)
+        scan(v("ss", 1, 49), v("na", 0, 48), v("ta", 0, 48), 0.0, A.mult, A.add)
+        for b in range(4):
+            ts(v("eoff", 2 * b, 2 * b + 2), v("ss", S, 49, S), 4.0, A.mult, float(b), A.add)
+        for b in range(4):
+            (act if b % 2 else copy)(v("et", b, 4 * L, 4), (v("xt"), v("eoff", 2 * b, 2 * b + 2)))
+        quant(qe, se, 0, 128, v("et"))
+        dst = T.cores[(rank + 1 + t) % N]
+        rid, pid = topo.addr(dst)[:2]
+        eng = topo.engines(core, dst)
+        half = len(eng) // 2
+        masks = [sum(1 << e for e in eng[:half]), sum(1 << e for e in eng[half:2 * half])]
+
+        def send(qt=qt, st=st, qe=qe, se=se, rid=rid, pid=pid, masks=masks, t=t):
+            to = [DstId(rid=rid, pnc=pid)]
+            return g.remote_dma_fused([
+                RemoteDMATransfer(dst_ids=to, dma_engine_mask=masks[0], remote_sem=T.sem["arr%d" % t],
+                                  src=T[qe][:, 0:L].bitcast(dt.uint8), dst=T[qt][:, C:B].bitcast(dt.uint8)),
+                RemoteDMATransfer(dst_ids=to, dma_engine_mask=masks[1], remote_sem=T.sem["arr%d" % t],
+                                  src=T[se][:, 0:128], dst=T[st][:, C:C + 128])], local_sem=T.sem.sent)
+
+        add("G", send, [v(qe), v(se)], [])
+        src = T.cores[(rank - 1 - t) % N]
+        ops.append({"q": None, "r": [], "w": [v(qt, C, B), v(st, C, C + 128)], "dma": False,
+                    "sig": ("arr%d" % t, len(topo.engines(src, core)) // 2 * 2)})
+
+        def carry(win, off, to):
+            cuts = [0, 384, 672, 960, 1248, 1536]
+            for j in range(5):
+                (act if j else copy)(v("b0", cuts[j], cuts[j + 1]), (win, v(off, cuts[j] // 16, cuts[j + 1] // 16)))
+            for j in range(5):
+                turn(v(to, cuts[j], cuts[j + 1]), v("b0", cuts[j], cuts[j + 1]))
+
+        def guests():
+            for b in range(4):
+                mx(5 - b % 2, "qi", "si", 128 * b, qt, st, B - 128, B)
+                act(v("bh", B * b + C, B * b + B), v("p%d" % (5 - b % 2), 128 - L, 128), scale=0.5)
+
+        if t == 0:
+            places()
+        if t >= EARLY:
+            for d in range(2):
+                copy(v("rin", 16 * d, 1536, 32), v("mm", 0, 48))
+                copy(v("rin", 16 * d + 1, 1536, 32), v("ss", 0, 48))
+            if t == EARLY:
+                for h in range(2):
+                    ts(v("rin", 768 * h + 2, 768 * h + 768, 16), v("capr"), 0.0, A.mult, col(GID + h), A.add)
+            turn(v("b2"), v("rin"))
+            unpack(t)
+            carry(v("b2"), "loff", "b1")
+            mx(4, "qu", "su", 0, qt, st, B - 128, B)
+            mx(5, "qp", "sp", 0, qt, st, B - 128, B)
+            copy(v("gwin", 0, L), v("p4", 128 - L, 128))
+            act(v("gwin", L, 2 * L), v("p5", 128 - L, 128))
+            carry(v("gwin"), "goff", "b3")
+            guests()
+            for u in range(2):
+                tt(v("vv", 48 * u, 48 * u + 48), v("b1", 16 * u, 1536, 32), v("b3", 16 * u, 1536, 32), A.max)
+            for u in range(2):
+                tt(v("tp", 48 * u, 48 * u + 48), v("b1", 16 * u, 1536, 32), v("b3", 16 * u, 1536, 32), A.is_le)
+            scan(v("m4", 1, 97), v("vv"), v("cap4"), -BIG, A.max, A.min)
+            for u in range(2):
+                tt(v("f1", 48 * u, 48 * u + 48), v("tp", 48 * u, 48 * u + 48), v("b1", 16 * u + 2, 1536, 32), A.mult)
+            tt(v("ab"), v("vv"), v("m4", 0, 96), A.is_gt)
+            for u in range(2):
+                tt(v("aa", 48 * u, 48 * u + 48), v("f1", 48 * u, 48 * u + 48), v("b1", 16 * u + 1, 1536, 32), A.max)
+            tt(v("na"), v("vv"), v("m4", 0, 96), A.is_le)
+            tt(v("ta"), v("aa"), v("ab"), A.mult)
+        else:
+            if t:
+                for d in range(2):
+                    copy(v("md", d, 96, 2), v("mm", 0, 48))
+                    copy(v("sd", d, 96, 2), v("ss", 0, 48))
+                unpack(t)
+            mx(4, "qp", "sp", 128, qt, st, B - 128, B)
+            tt(v("gm"), v("p4", 128 - L, 128), v("capg"), A.min)
+            guests()
+            for h in range(2):
+                rmax(v("gg", h, h + 1), v("gm", 16 * h, 16 * h + 16))
+            for h in range(2):
+                ts(v("tp", 48 * h, 48 * h + 48), v("md", 48 * h, 48 * h + 48), v("gg", h, h + 1), A.is_le, col(GID + h), A.mult)
+            for h in range(2):
+                ts(v("rin", 768 * h, 768 * h + 768, 16), v("md", 48 * h, 48 * h + 48), v("gg", h, h + 1), A.max)
+            tt(v("rin", 1, 1536, 16), v("tp"), v("sd"), A.max)
+            turn(v("b2"), v("rin"))
+            if t == 0:
+                walked()
+            carry(v("b2"), "loff", "b1")
+            for u in range(2):
+                scan(v("m4", 1 + 48 * u, 49 + 48 * u), v("b1", 16 * u, 1536, 32), v("cap4", 0, 48), -BIG, A.max, A.min)
+            for u in range(2):
+                tt(v("ab", 48 * u, 48 * u + 48), v("b1", 16 * u, 1536, 32), v("m4", 48 * u, 48 * u + 48), A.is_gt)
+            for u in range(2):
+                tt(v("na", 48 * u, 48 * u + 48), v("b1", 16 * u, 1536, 32), v("m4", 48 * u, 48 * u + 48), A.is_le)
+            for u in range(2):
+                tt(v("ta", 48 * u, 48 * u + 48), v("b1", 16 * u + 1, 1536, 32), v("ab", 48 * u, 48 * u + 48), A.mult)
+        scan(v("s4"), v("na"), v("ta"), 0.0, A.mult, A.add)
+        for u in range(2):
+            copy(v("aoff", u, 24, 2), v("s4", 48 * u + 3, 48 * u + 48, 4))
+        for c in range(2):
+            off = v("aoff", 12 * c, 12 * c + 12)
+            for b in range(2):
+                act(v("pb", C * b + H * c, C * b + H * c + H), (v("bh", B * (b + 2), B * (b + 3)), off))
+        if t == R - 1:
+            act(v("oar"), (v("jrow"), v("aoff")))
+            dma("Y", T.oa[:], T.oar[0:128:16, :], [v("oar")], [])
+        for c in range(2):
+            off = v("aoff", 12 * c, 12 * c + 12)
+            for b in range(2):
+                tt(v("yt", 4 * H * c + b, 4 * H * (c + 1), 4), (v("bh", B * b, B * b + B), off), v("fh", C * b + H * c, C * b + H * c + H), A.add)
+            for b in range(2):
+                tt(v("yt", 4 * H * c + b + 2, 4 * H * (c + 1), 4), v("pb", C * b + H * c, C * b + H * c + H), v("p%d" % (6 + b), H * c, H * c + H), A.add)
+            quant("qy", "sy", H * c, H * c + H, v("yt", 4 * H * c, 4 * H * (c + 1)))
+            for b in range(4):
+                mx(4 + b % 2, "qw", "sw", 128 * b, "qy", "sy", H * c, H * c + H)
+                act(v("rr", C * b + H * c, C * b + H * c + H), v("p%d" % (4 + b % 2), 0, H), F.Relu, 2.0 ** -5)
+        qn, sn = "qt%d" % (t + 1), "st%d" % (t + 1)
+        for c in range(2):
+            for b in range(4):
+                tt(v("xt", 4 * H * c + b, 4 * H * (c + 1), 4), v("rr", C * b + H * c, C * b + H * c + H), v("p%d" % b, H * c, H * c + H), A.add)
+            quant(qn, sn, H * c, H * c + H, v("xt", 4 * H * c, 4 * H * (c + 1)))
+            if t < R - 1:
+                scores(t + 1, c)
+                if c == 1 and t == EARLY - 1:
+                    copy(v("i2"), v("loff"))
+                    ts(col(U32), col(U), float(L), A.mult)
+                    ts(col(N32), col(U), -float(L), A.mult, float(L), A.add)
+                    ts(v("i3"), v("i2"), 15, A.bitwise_and)
+                    ts(v("f1"), v("i2"), 768.0, A.is_ge, 16.0, A.mult)
+                    tt(v("f2"), v("f1"), v("i3"), A.add)
+                    ts(v("goff", 0, 96, 2), v("f2", 0, 96, 2), col(U32), A.add)
+                    ts(v("goff", 1, 96, 2), v("f2", 1, 96, 2), col(N32), A.add)
+                if c == 1 and t == 1:
+                    quant("qv", "sv", 0, 128, v("vt"))
+            else:
+                mx(4 + c, "qv", "sv", 0, qn, sn, H * c, H * c + H)
+                dma("Y", T.oc[:, 4 * H * c:4 * H * (c + 1)], ap(v(qn, H * c, H * c + H)).bitcast(dt.uint8), [v(qn, H * c, H * c + H)], [])
+                act(v("yo", H * c, H * c + H), v("p%d" % (4 + c), 0, H))
+                dma("A", T.y[:, H * c:H * c + H], ap(v("yo", H * c, H * c + H)), [v("yo", H * c, H * c + H)], [])
+    for k in range(4):
+        dma("Y", T.osc[4 * k:4 * k + 4, :], T["st%d" % R][32 * k:32 * k + 4, 0:C], [v("st%d" % R, 0, C)], [])
+    _emit(g, T, ops)
+    g.wait_ge(T.sem.sent, sum(len(topo.engines(core, T.cores[(rank + 1 + t) % N])) // 2 * 2 for t in range(R)))

@@ -1,13 +1,12 @@
 from concourse.bass import DstId, RemoteDMATransfer
-from concourse.mybir import dt, AluOpType, AxisListType, ActivationFunctionType
+from concourse.mybir import dt, AluOpType, ActivationFunctionType
 
 C, L, S, R = 384, 32, 24, 3
 H = C // 2
 B = C + L
 BIG = 1e29
 CODE = "float8_e4m3fn_x4"
-IN_ORDER = True
-EARLY = 1
+CUTS = (0, 224, 416, 768, 1088, 1344, 1536)
 
 
 def _sb(n, d="float32"):
@@ -20,19 +19,21 @@ SCRATCH = {
     "fh": _sb(2 * C, "bfloat16"), "jb": _sb(12),
     "ones": _sb(516, "bfloat16"), "ida": _sb(516, "bfloat16"), "idb": _sb(516, "bfloat16"), "idh": _sb(1024, "bfloat16"),
     "cap16": _sb(C, "bfloat16"),
-    "qu": _sb(128, CODE), "su": _sb(128, "uint8"), "qp": _sb(256, CODE), "sp": _sb(256, "uint8"),
+    "qu": _sb(128, CODE), "su": _sb(128, "uint8"), "qp": _sb(128, CODE), "sp": _sb(128, "uint8"),
     "qv": _sb(128, CODE), "sv": _sb(128, "uint8"), "qw": _sb(512, CODE), "sw": _sb(512, "uint8"),
     "qi": _sb(768, CODE), "si": _sb(768, "uint8"), "qy": _sb(C, CODE), "sy": _sb(C, "uint8"),
     "rti": _sb(48, "int32"), "fti": _sb(24, "int32"), "rowi": _sb(768, "int32"),
     "ci": _sb(8, "int32"), "cf": _sb(16), "i1": _sb(144), "i2": _sb(96, "int32"), "i3": _sb(96, "int32"),
-    "i4": _sb(96, "int32"), "iu": _sb(16, "int32"), "fld": _sb(576, "int32"), "eq": _sb(32), "capg": _sb(32),
+    "i4": _sb(96, "int32"), "iu": _sb(8, "int32"), "fld": _sb(576, "int32"), "eq": _sb(16), "i16": _sb(16),
     "capr": _sb(48), "cap4": _sb(96), "jrow": _sb(B), "tab": _sb(576), "key": _sb(96), "sums": _sb(12),
-    "uoff": _sb(16, "uint16"), "koff": _sb(96, "uint16"), "zoff": _sb(48, "uint16"), "roff": _sb(48, "uint16"),
+    "uoff": _sb(8, "uint16"), "koff": _sb(96, "uint16"), "zoff": _sb(48, "uint16"), "roff": _sb(48, "uint16"),
     "foff": _sb(24, "uint16"), "coff": _sb(48, "uint16"), "loff": _sb(96, "uint16"), "eoff": _sb(8, "uint16"),
-    "aoff": _sb(24, "uint16"), "goff": _sb(96, "uint16"), "gwin": _sb(2 * L), "vv": _sb(96), "aa": _sb(96),
+    "aoff": _sb(24, "uint16"), "goff": _sb(96, "uint16"), "gwin": _sb(2 * L), "vv": _sb(96),
     "way": _sb(48), "wrow": _sb(768), "swin": _sb(768), "b0": _sb(1536), "b1": _sb(1536), "b2": _sb(1536), "b3": _sb(1536),
-    "rin": _sb(1536), "rr": _sb(4 * C), "mm": _sb(49), "ss": _sb(49), "ab": _sb(96), "na": _sb(96), "ta": _sb(96),
-    "md": _sb(96), "sd": _sb(96), "gm": _sb(32), "gg": _sb(2), "tp": _sb(96), "m4": _sb(97), "s4": _sb(96),
+    "rin": _sb(1536), "rr": _sb(4 * C), "mm": _sb(49), "ss": _sb(98), "na": _sb(96),
+    "w0": _sb(96), "w1": _sb(96), "g0": _sb(192), "g1": _sb(192), "g2": _sb(192),
+    "md": _sb(96), "sd": _sb(96), "gg": _sb(64), "q4": _sb(4), "tp": _sb(96), "m4": _sb(97), "s4": _sb(96),
+    "e0": _sb(288), "e1": _sb(288), "e2": _sb(288),
     "f1": _sb(96), "f2": _sb(96), "yo": _sb(C), "oar": _sb(C),
 }
 for _t in range(R + 1):
@@ -44,9 +45,7 @@ for _t in range(R):
 for _b in range(8):
     SCRATCH["p%d" % _b] = ("psum", [128, 512], "float32")
 
-POOL = {"V": 50, "A": 30, "P": 20, "G": 10}
-SEMAPHORES = (["sent"] + ["arr%d" % t for t in range(R)] + ["d%d" % i for i in range(30)]
-              + ["%s%d" % (e.lower(), i) for e in POOL for i in range(1 if IN_ORDER else POOL[e])])
+SEMAPHORES = ["sent", "v", "a", "p", "g"] + ["arr%d" % t for t in range(R)] + ["d%d" % i for i in range(24)]
 
 
 def _mask(v):
@@ -92,10 +91,10 @@ def _emit(g, T, ops):
                 k.add(d)
                 k |= ops[d]["known"]
         o["known"] = set(k)
-        if IN_ORDER and not o["dma"]:
+        if not o["dma"]:
             o["known"] |= set(earlier[o["q"]])
             earlier[o["q"]].append(n)
-    count, turn, dmas, last = {}, {q: 0 for q in queue}, 0, []
+    count, dmas, last = {}, 0, []
     for o in ops:
         if o["q"] is None:
             continue
@@ -110,8 +109,7 @@ def _emit(g, T, ops):
             if not o.get("needed"):
                 last.append((q, o["sig"]))
         elif o.get("needed"):
-            name = "%s%d" % (o["q"].lower(), 0 if IN_ORDER else turn[o["q"]] % POOL[o["q"]])
-            turn[o["q"]] += 1
+            name = o["q"].lower()
             count[name] = count.get(name, 0) + 1
             o["sig"] = (name, count[name])
             ins.then_inc(T.sem[name], 1)
@@ -169,18 +167,18 @@ def rank_program(g, core, T, topo):
     def turn(o, i):
         add("V", lambda: g.vector.transpose(ap(o), ap(i)), [i], [o])
 
-    def rmax(o, i):
-        add("V", lambda: g.vector.tensor_reduce(ap(o), ap(i), AxisListType.X, A.max), [i], [o])
-
     def act(o, i, func=F.Copy, scale=1.0, acc=None, bias=None):
         if bias is not None:
-            add("A", lambda: g.scalar.activation(ap(o), ap(i), func, bias=ap(bias)), rd(i, bias), [o])
+            add("A", lambda: g.scalar.activation(ap(o), ap(i), func, bias=ap(bias), scale=scale), rd(i, bias), [o])
         elif SCRATCH[o[0]][2] == "uint8":
             add("A", lambda: g.scalar.activation(ap(o), ap(i), func), rd(i), [o])
         elif acc is None:
             add("A", lambda: g.scalar.activation(ap(o), ap(i), func, scale=scale), rd(i), [o])
         else:
             add("A", lambda: g.scalar.activation(ap(o), ap(i), func, accum_out=ap(acc)), rd(i), [o, acc])
+
+    def other(o, i):
+        act(o, i, F.Identity, -1.0, bias=v("ones", 0, 1))
 
     def const(o, c):
         act(o, v("ones", 0, len(range(*o[1:]))), scale=c)
@@ -210,62 +208,60 @@ def rank_program(g, core, T, topo):
 
     fill(v("rowi"), 0)
     dma("Y", T.rti[:], T.rt[:], [], [v("rti")])
-    dma("Y", T.ut[:], T.u[:], [], [v("ut")])
+    dma("A", T.ut[:], T.u[:], [], [v("ut")])
     dma("Y", T.rowi[0:128:16, :], T.rt[:], [], [v("rowi")])
     for c in range(2):
         dma("Y", ap(v("xt", 4 * H * c, 4 * H * (c + 1))), T.x[:, 4 * H * c:4 * H * (c + 1)], [], [v("xt", 4 * H * c, 4 * H * (c + 1))])
     iota(v("ci", 0, 1), [[0, 1]], 0, 1)
     iota(v("i1", 0, 48), [[384, 2], [1, 24]])
-    iota(v("capg"), [[0, 2], [1, 16]])
-    iota(v("iu", 0, 8), [[32, 4], [-16, 2]], 16)
+    iota(v("i16"), [[1, 16]])
+    iota(v("iu"), [[32, 4], [-16, 2]], 16)
     iota(v("i1", 48, 96), [[1, 16], [256, 3]])
-    iota(v("iu", 8, 16), [[16, 8]])
     iota(v("i1", 96, 144), [[16, 48]])
     iota(v("jb"), [[32, 12]])
     fill(v("ones"), 1.0)
     for name, base in (("ida", 2), ("idb", 3)):
         add("G", lambda name=name, base=base: g.affine_select(T[name][:], T.ones[:], [[-1, 516]], A.is_equal, 0.0, base, 4),
             [v("ones")], [v(name)])
+    iota(v("et", 4 * L, 512), [[0, 512 - 4 * L]])
     iota(v("jrow"), [[1, B]])
     ts(v("ci", 2, 3), v("ci", 0, 1), 15, A.bitwise_and)
     ts(v("ci", 3, 4), v("ci", 0, 1), 4, A.logical_shift_right, 1, A.bitwise_and)
     const(v("tab", 0, H), 0.0)
     const(v("tab", C, C + H), 0.0)
-    const(v("capr"), BIG)
-    const(v("mm", 0, 1), -BIG)
-    const(v("m4", 0, 1), -BIG)
-    const(v("ss", 0, 1), 0.0)
-    const(v("capr", S - 1, 48, S), -BIG)
     copy(v("cf", 0, 2), v("ci", 2, 4))
     ts(col(K24), col(K), 24.0, A.mult)
-    ts(v("eq"), v("capg"), col(K), A.is_equal)
+    ts(v("eq"), v("i16"), col(K), A.is_equal)
     ts(col(K16), col(K), 16.0, A.mult)
     ts(v("i2", 0, 48), v("i1", 0, 48), col(K24), A.add)
     ts(col(U384), col(U), float(C), A.mult)
+    ts(col(N384), col(U), -float(C), A.mult, float(C), A.add)
     ts(v("i3", 0, 48), v("i2", 0, 48), 15, A.bitwise_and)
     ts(v("i4", 0, 48), v("i2", 0, 48), 4, A.logical_shift_right)
     for m in range(12):
-        act(v("tab", H + 16 * m, H + 16 * m + 16), v("eq", 0, 16), scale=4.0 ** (3 * (m % 4) + m // 4))
+        act(v("tab", H + 16 * m, H + 16 * m + 16), v("eq"), scale=4.0 ** (3 * (m % 4) + m // 4))
+    const(v("capr"), BIG)
+    for b in range(4):
+        const(v("q4", b, b + 1), b / 4)
+    const(v("mm", 0, 1), -BIG)
+    const(v("m4", 0, 1), -BIG)
+    const(v("ss", 1, 2), 0.0)
+    const(v("w0", 0, 96, 2), 1.0)
+    const(v("capr", S - 1, 48, S), -BIG)
+    ts(col(GID), col(K), float(C), A.add)
     ts(v("i3", 0, 48), v("i3", 0, 48), 48.0, A.mult)
-    ts(col(N384), col(U), -float(C), A.mult, float(C), A.add)
+    ts(col(GID + 1), col(K), float(C + 16), A.add)
+    ts(col(C32), col(U), 16.0, A.mult, col(K), A.add)
     tt(v("i2", 0, 48), v("i3", 0, 48), v("i4", 0, 48), A.add)
     copy(v("uoff"), v("iu"))
-    copy(v("koff", 0, 48), v("i2", 0, 48))
     ts(v("koff", 48, 96), v("i1", 48, 96), col(K16), A.add)
-    ts(col(GID), col(K), float(C), A.add)
-    ts(col(GID + 1), col(K), float(C + 16), A.add)
-    ts(v("capg"), v("eq"), 2 * BIG, A.mult, -BIG, A.add)
-    ts(v("f2", 0, 48), v("i1", 96, 144), col(K), A.add)
-    ts(col(C32), col(U), 16.0, A.mult, col(K), A.add)
+    copy(v("koff", 0, 48), v("i2", 0, 48))
     copy(v("roff"), v("rti"))
+    ts(col(U32), col(U), float(L), A.mult)
+    ts(col(N32), col(U), -float(L), A.mult, float(L), A.add)
+    ts(v("f2", 0, 48), v("i1", 96, 144), col(K), A.add)
     ts(v("jb"), v("jb"), col(C32), A.add, -2048.0, A.mult)
     quant("qu", "su", 0, 128, v("ut"))
-
-    def pick(a):
-        o, off = v("qp", a, a + 128), v("uoff", a // 16, a // 16 + 8)
-        add("V", lambda: g.vector.tensor_copy(ap(o).bitcast(dt.uint32), T.qu[:, 0:128].bitcast(dt.uint32).indirect(ap(off))),
-            [v("qu"), off], [o])
-        act(v("sp", a, a + 128), (v("su"), off))
 
     def counts(p):
         act(v("b2", 768 * p, 768 * p + 768), (v("tab", H * (1 - p), H * (1 - p) + C), v("roff")))
@@ -276,11 +272,13 @@ def rank_program(g, core, T, topo):
 
     copy(v("b0", 0, 768), (v("rowi"), v("koff", 0, 48)))
     counts(0)
-    pick(0)
+    add("V", lambda: g.vector.tensor_copy(T.qp[:, 0:128].bitcast(dt.uint32), T.qu[:, 0:128].bitcast(dt.uint32).indirect(T.uoff[:, 0:8])),
+        [v("qu"), v("uoff")], [v("qp")])
+    act(v("sp"), (v("su"), v("uoff")))
     act(v("wrow"), (v("b0", 0, 768), v("koff", 48, 96)))
     dma("Y", T.way[:], T.wrow[0:128:16, :], [v("wrow")], [v("way")])
     dma("Y", T.fti[:], T.ft[:], [], [v("fti")])
-    dma("Y", T.qw[:].bitcast(dt.uint8), T.wc[:], [], [v("qw")])
+    dma("Y", T.qw[:].bitcast(dt.uint8), T.wc[:], [v("way")], [v("qw")])
     dma("Y", T.sw[:], T.ws[:], [], [v("sw")])
     dma("Y", T.vt[:], T.v[:], [], [v("vt")])
 
@@ -290,24 +288,30 @@ def rank_program(g, core, T, topo):
         act(v("swin", H * c, H * c + H), v("p%d" % (4 + 2 * c), 0, H))
         (act if c == 0 or t == 0 else copy)(v("swin", C + H * c, C + H * c + H), v("p%d" % (5 + 2 * c), 0, H))
 
+    turn(v("b1", 0, 768), v("b0", 0, 768))
     for c in range(2):
         quant("qt0", "st0", H * c, H * c + H, v("xt", 4 * H * c, 4 * H * (c + 1)))
         scores(0, c)
-    turn(v("b1", 0, 768), v("b0", 0, 768))
     ts(v("zoff", 0, 48, 2), v("b1", 0, 768, 32), col(U384), A.add)
     ts(v("zoff", 1, 48, 2), v("b1", 16, 768, 32), col(N384), A.add)
     running(0)
 
     def places():
         running(1)
+        for d in range(2):
+            act(v("md", d, 96, 2), v("mm", 0, 48))
+            act(v("sd", d, 96, 2), v("ss", 1, 97, 2))
         const(v("cap16"), -1.0)
         const(v("cap4"), BIG)
         for b in range(2):
             act(v("idh", 512 * b, 512 * b + 512), v("idb" if b else "ida", 0, 512), scale=0.5)
         const(v("cap16", 0, C, 16), 2.0 ** 21)
         const(v("cap4", 3, 96, 4), -BIG)
+        tt(v("f1", 48, 96), v("f1", 0, 48), v("f2", 0, 48), A.subtract)
+        tt(v("key", 0, 48), v("f1", 0, 48), v("f2", 0, 48), A.add)
         copy(v("i2"), v("rin", 15, 1536, 16))
-        ts(v("f1", 0, 48), v("rti"), 2048.0, A.mult)
+        ts(v("key", 48, 96), v("f1", 48, 96), 1023.0, A.add)
+        copy(v("foff"), v("fti"))
         for r in range(6):
             ts(v("fld", 96 * r, 96 * r + 96), v("i2"), r, A.logical_shift_right, 0x041041, A.bitwise_and)
         for h in range(2):
@@ -316,34 +320,25 @@ def rank_program(g, core, T, topo):
                 for p in range(2):
                     j = 6 * (r % 2) + 3 * p + r // 2
                     act(v("b1", 48 * j, 48 * j + 48), v("b0", 96 * r + 48 * p, 96 * r + 48 * p + 48), acc=v("sums", j, j + 1))
-        tt(v("key", 0, 48), v("f1", 0, 48), v("f2", 0, 48), A.add)
-        tt(v("f1", 48, 96), v("f1", 0, 48), v("f2", 0, 48), A.subtract)
-        copy(v("foff"), v("fti"))
-        ts(v("key", 48, 96), v("f1", 48, 96), 1023.0, A.add)
-        for b in range(2):
-            quant("qi", "si", 128 * b, 128 * b + 128, v("idb" if b % 2 else "ida", 2, 514))
+        quant("qi", "si", 512, 768, v("idh"))
+        ident(0, 2)
+        ident(0, 3)
         copy(v("i3", 0, 12), v("sums"))
         for f in range(4):
             ts(v("i4", f, 48, 4), v("i3", 0, 12), 6 * f, A.logical_shift_right, 63, A.bitwise_and)
         tt(v("i4", 0, 24), v("i4", 0, 24), v("i4", 24, 48), A.add)
-        for p in range(2):
+        for p in (1, 0):
             for h in range(2):
                 ts(v("coff", 2 * p + h, 48, 4), v("i4", 24 * p + h, 24 * p + 24, 2), -1.0, A.mult, 48.0 * (p + 1), A.add)
-        for p in range(2):
-            act(v("b0", C * p, C * p + C), (v("key"), v("coff", 24 * p, 24 * p + 24)))
-        for b in range(2, 4):
-            quant("qi", "si", 128 * b, 128 * b + 128, v("idb" if b % 2 else "ida", 0, 512))
-        quant("qi", "si", 512, 768, v("idh"))
-        turn(v("b1", 0, C), v("b0", 0, C))
-        for d in range(2):
-            copy(v("md", d, 96, 2), v("mm", 0, 48))
-            copy(v("sd", d, 96, 2), v("ss", 0, 48))
-        turn(v("b1", C, 2 * C), v("b0", C, 2 * C))
+        act(v("b0", C, 2 * C), (v("key"), v("coff", 24, 48)))
+        copy(v("b0", 0, H), (v("key"), v("coff", 0, 12)))
+        copy(v("b0", H, C), (v("key"), v("coff", 12, 24)))
+        for j in range(4):
+            turn(v("b1", H * j, H * j + H), v("b0", H * j, H * j + H))
         for b in range(12):
             act(v("b2", 64 * b, 64 * b + 64), v("b1", 64 * b, 64 * b + 64), F.Abs, bias=v("jb", b, b + 1))
-        for p in range(2):
-            scan(v("b3", C * p, C * p + C), v("cap16"), v("b2", C * p, C * p + C), 0.0, A.max, A.min)
-        pick(128)
+        for j in range(4):
+            scan(v("b3", H * j, H * j + H), v("cap16", 0, H), v("b2", H * j, H * j + H), 0.0, A.max, A.min)
         unpack(0)
         for h in range(2):
             copy(v("i2", h, 24, 2), v("b3", 15 + 16 * h, 2 * C, 64))
@@ -359,46 +354,53 @@ def rank_program(g, core, T, topo):
         for p in range(2):
             tt(v("b0", p, C, 16), v("f1", 48 + 24 * p, 72 + 24 * p), v("f2", 48 + 24 * p, 72 + 24 * p), A.add)
         turn(v("b1", 0, C), v("b0", 0, C))
-        act(v("wrow", 0, C), (v("b1", 0, C), v("foff")))
-        for p in range(2):
-            for h in range(2):
-                copy(v("loff", 2 * p + h, 96, 8), v("b0", 16 * h + p, C, 32))
 
-    def walked():
-        turn(v("b3", 0, C), v("wrow", 0, C))
-        for p in range(2):
-            for h in range(2):
-                copy(v("loff", 4 + 2 * p + h, 96, 8), v("b3", 16 * h + p, C, 32))
+    def ident(t, b):
+        if t == 0:
+            quant("qi", "si", 128 * b, 128 * b + 128, v("idb" if b % 2 else "ida", 2 - b // 2 * 2, 514 - b // 2 * 2))
 
     def unpack(t):
         for b in range(4):
             mx(b, "qi", "si", 128 * b, "qt%d" % t, "st%d" % t, 0, C)
-            act(v("bh", B * b, B * b + C), v("p%d" % b, 0, C), scale=0.5)
             if b < 2:
+                act(v("bh", B * b, B * b + C), v("p%d" % b, 0, C), scale=0.5)
                 act(v("fh", C * b, C * b + C), v("p%d" % b, 0, C), scale=0.5)
         for b in range(2):
             mx(6 + b, "qi", "si", 512 + 128 * b, "qt%d" % t, "st%d" % t, 0, C)
 
+    def rest():
+        for b in range(2, 4):
+            act(v("bh", B * b, B * b + C), v("p%d" % b, 0, C), scale=0.5)
+
+    def carry(win, off, to, cuts=CUTS):
+        for j in range(len(cuts) - 1):
+            (act if j > 1 else copy)(v("b0", cuts[j], cuts[j + 1]), (win, v(off, cuts[j] // 16, cuts[j + 1] // 16)))
+        for j in range(len(cuts) - 1):
+            turn(v(to, cuts[j], cuts[j + 1]), v("b0", cuts[j], cuts[j + 1]))
+
     for t in range(R):
         qt, st, qe, se = "qt%d" % t, "st%d" % t, "qe%d" % t, "se%d" % t
-        for j in range(2):
-            act(v("b0", 256 * j, 256 * j + 256), (v("swin"), v("zoff", 16 * j, 16 * j + 16)))
-        copy(v("b0", 512, 768), (v("swin"), v("zoff", 32, 48)))
-        for j in (2, 0, 1):
-            turn(v("b1", 256 * j, 256 * j + 256), v("b0", 256 * j, 256 * j + 256))
+        carry(v("swin"), "zoff", "b1", (0, 128, 256, 512, 768))
         z = v("b1", 0, 768, 16)
         if t == 0:
-            const(v("et", 4 * L, 512), 0.0)
+            act(v("w1", 0, 96, 2), v("way"), scale=-1.0)
+            act(v("w1", 1, 96, 2), v("way"))
             counts(1)
         scan(v("mm", 1, 49), z, v("capr"), -BIG, A.max, A.min)
-        tt(v("ab", 0, 48), z, v("mm", 0, 48), A.is_gt)
-        tt(v("na", 0, 48), z, v("mm", 0, 48), A.is_le)
-        tt(v("ta", 0, 48), v("ab", 0, 48), v("way"), A.mult)
-        scan(v("ss", 1, 49), v("na", 0, 48), v("ta", 0, 48), 0.0, A.mult, A.add)
+        ident(t, 0)
+        tt(v("w0", 1, 96, 2), z, v("mm", 0, 48), A.is_le)
+        ident(t, 1)
+        for d in range(2 if t else 0):
+            act(v("rin", 16 * d, 1536, 32), v("mm", 0, 48))
+        scan(v("ss", 2, 98), v("w0"), v("w1"), 0.0, A.mult, A.add)
+        if t == 0:
+            ts(v("f1", 0, 48), v("rti"), 2048.0, A.mult)
+        for h in range(2):
+            ts(v("eoff", h, 8, 2), v("q4"), v("ss", 2 * S * (h + 1) + 1, 2 * S * (h + 1) + 2), A.add, 4.0, A.mult)
+        for d in range(2 if t else 0):
+            act(v("rin", 16 * d + 1, 1536, 32), v("ss", 1, 97, 2))
         for b in range(4):
-            ts(v("eoff", 2 * b, 2 * b + 2), v("ss", S, 49, S), 4.0, A.mult, float(b), A.add)
-        for b in range(4):
-            (act if b % 2 else copy)(v("et", b, 4 * L, 4), (v("xt"), v("eoff", 2 * b, 2 * b + 2)))
+            (act if b % 2 and t else copy)(v("et", b, 4 * L, 4), (v("xt"), v("eoff", 2 * b, 2 * b + 2)))
         quant(qe, se, 0, 128, v("et"))
         dst = T.cores[(rank + 1 + t) % N]
         rid, pid = topo.addr(dst)[:2]
@@ -419,120 +421,134 @@ def rank_program(g, core, T, topo):
         ops.append({"q": None, "r": [], "w": [v(qt, C, B), v(st, C, C + 128)], "dma": False,
                     "sig": ("arr%d" % t, len(topo.engines(src, core)) // 2 * 2)})
 
-        def carry(win, off, to):
-            cuts = [0, 384, 672, 960, 1248, 1536]
-            for j in range(5):
-                (act if j else copy)(v("b0", cuts[j], cuts[j + 1]), (win, v(off, cuts[j] // 16, cuts[j + 1] // 16)))
-            for j in range(5):
-                turn(v(to, cuts[j], cuts[j + 1]), v("b0", cuts[j], cuts[j + 1]))
-
         def guests():
             for b in range(4):
                 mx(5 - b % 2, "qi", "si", 128 * b, qt, st, B - 128, B)
                 act(v("bh", B * b + C, B * b + B), v("p%d" % (5 - b % 2), 128 - L, 128), scale=0.5)
 
-        if t == 0:
-            places()
-        if t >= EARLY:
-            for d in range(2):
-                copy(v("rin", 16 * d, 1536, 32), v("mm", 0, 48))
-                copy(v("rin", 16 * d + 1, 1536, 32), v("ss", 0, 48))
-            if t == EARLY:
-                for h in range(2):
-                    ts(v("rin", 768 * h + 2, 768 * h + 768, 16), v("capr"), 0.0, A.mult, col(GID + h), A.add)
+        if t:
             turn(v("b2"), v("rin"))
+            if t == 1:
+                copy(v("i2"), v("loff"))
+                quant("qv", "sv", 0, 128, v("vt"))
             unpack(t)
             carry(v("b2"), "loff", "b1")
+            for u in range(2):
+                act(v("e1", 144 * u + 1, 144 * u + 144, 3), v("b1", 16 * u + 1, 1536, 32))
+            if t == 1:
+                for u in range(2):
+                    act(v("e1", 144 * u, 144 * u + 144, 3), v("b1", 16 * u + 2, 1536, 32))
+                ts(v("f1"), v("i2"), 768.0, A.is_ge, 16.0, A.mult)
+                ts(v("i3"), v("i2"), 15, A.bitwise_and)
+                tt(v("f2"), v("f1"), v("i3"), A.add)
+                ts(v("goff", 0, 96, 2), v("f2", 0, 96, 2), col(U32), A.add)
+                ts(v("goff", 1, 96, 2), v("f2", 1, 96, 2), col(N32), A.add)
             mx(4, "qu", "su", 0, qt, st, B - 128, B)
             mx(5, "qp", "sp", 0, qt, st, B - 128, B)
-            copy(v("gwin", 0, L), v("p4", 128 - L, 128))
-            act(v("gwin", L, 2 * L), v("p5", 128 - L, 128))
+            act(v("gwin", 0, L), v("p4", 128 - L, 128))
+            copy(v("gwin", L, 2 * L), v("p5", 128 - L, 128))
             carry(v("gwin"), "goff", "b3")
             guests()
+            rest()
             for u in range(2):
                 tt(v("vv", 48 * u, 48 * u + 48), v("b1", 16 * u, 1536, 32), v("b3", 16 * u, 1536, 32), A.max)
-            for u in range(2):
-                tt(v("tp", 48 * u, 48 * u + 48), v("b1", 16 * u, 1536, 32), v("b3", 16 * u, 1536, 32), A.is_le)
+            tt(v("e0", 1, 144, 3), v("b1", 0, 1536, 32), v("b3", 0, 1536, 32), A.is_le)
             scan(v("m4", 1, 97), v("vv"), v("cap4"), -BIG, A.max, A.min)
-            for u in range(2):
-                tt(v("f1", 48 * u, 48 * u + 48), v("tp", 48 * u, 48 * u + 48), v("b1", 16 * u + 2, 1536, 32), A.mult)
-            tt(v("ab"), v("vv"), v("m4", 0, 96), A.is_gt)
-            for u in range(2):
-                tt(v("aa", 48 * u, 48 * u + 48), v("f1", 48 * u, 48 * u + 48), v("b1", 16 * u + 1, 1536, 32), A.max)
-            tt(v("na"), v("vv"), v("m4", 0, 96), A.is_le)
-            tt(v("ta"), v("aa"), v("ab"), A.mult)
+            tt(v("e0", 145, 288, 3), v("b1", 16, 1536, 32), v("b3", 16, 1536, 32), A.is_le)
+            tt(v("e0", 2, 288, 3), v("vv"), v("m4", 0, 96), A.is_gt)
+            other(v("na"), v("e0", 2, 288, 3))
+            scan(v("e2"), v("e0"), v("e1"), 0.0, A.mult, A.max)
+            scan(v("s4"), v("na"), v("e2", 2, 288, 3), 0.0, A.mult, A.add)
         else:
-            if t:
-                for d in range(2):
-                    copy(v("md", d, 96, 2), v("mm", 0, 48))
-                    copy(v("sd", d, 96, 2), v("ss", 0, 48))
-                unpack(t)
-            mx(4, "qp", "sp", 128, qt, st, B - 128, B)
-            tt(v("gm"), v("p4", 128 - L, 128), v("capg"), A.min)
+            places()
+            mx(4, "qu", "su", 0, qt, st, B - 128, B)
+            mx(5, "qp", "sp", 0, qt, st, B - 128, B)
+            act(v("wrow", 0, C), (v("b1", 0, C), v("foff")))
+            for p in range(2):
+                for h in range(2):
+                    copy(v("loff", 2 * p + h, 96, 8), v("b0", 16 * h + p, C, 32))
+            for h in range(2):
+                copy(v("gwin", 32 * h, 32 * h + 16), v("p4", 96 + 16 * h, 112 + 16 * h))
+            for h in range(2):
+                copy(v("gwin", 32 * h + 16, 32 * h + 32), v("p5", 96 + 16 * h, 112 + 16 * h))
+            turn(v("b3", 0, C), v("wrow", 0, C))
+            turn(v("gg"), v("gwin"))
             guests()
+            for p in range(2):
+                for h in range(2):
+                    copy(v("loff", 4 + 2 * p + h, 96, 8), v("b3", 16 * h + p, C, 32))
             for h in range(2):
-                rmax(v("gg", h, h + 1), v("gm", 16 * h, 16 * h + 16))
+                ts(v("tp", 48 * h, 48 * h + 48), v("md", 48 * h, 48 * h + 48), v("gg", 32 * h, 32 * h + 1), A.is_le, col(GID + h), A.mult)
             for h in range(2):
-                ts(v("tp", 48 * h, 48 * h + 48), v("md", 48 * h, 48 * h + 48), v("gg", h, h + 1), A.is_le, col(GID + h), A.mult)
-            for h in range(2):
-                ts(v("rin", 768 * h, 768 * h + 768, 16), v("md", 48 * h, 48 * h + 48), v("gg", h, h + 1), A.max)
+                ts(v("rin", 768 * h, 768 * h + 768, 16), v("md", 48 * h, 48 * h + 48), v("gg", 32 * h, 32 * h + 1), A.max)
             tt(v("rin", 1, 1536, 16), v("tp"), v("sd"), A.max)
             turn(v("b2"), v("rin"))
-            if t == 0:
-                walked()
+            const(v("e0", 0, 288, 3), 0.0)
+            const(v("e1", 2, 288, 3), 0.0)
+            const(v("g0", 0, 192, 2), 1.0)
+            rest()
             carry(v("b2"), "loff", "b1")
             for u in range(2):
                 scan(v("m4", 1 + 48 * u, 49 + 48 * u), v("b1", 16 * u, 1536, 32), v("cap4", 0, 48), -BIG, A.max, A.min)
             for u in range(2):
-                tt(v("ab", 48 * u, 48 * u + 48), v("b1", 16 * u, 1536, 32), v("m4", 48 * u, 48 * u + 48), A.is_gt)
+                act(v("g1", 96 * u, 96 * u + 96, 2), v("b1", 16 * u + 1, 1536, 32), scale=-1.0)
+                act(v("g1", 96 * u + 1, 96 * u + 96, 2), v("b1", 16 * u + 1, 1536, 32))
             for u in range(2):
-                tt(v("na", 48 * u, 48 * u + 48), v("b1", 16 * u, 1536, 32), v("m4", 48 * u, 48 * u + 48), A.is_le)
-            for u in range(2):
-                tt(v("ta", 48 * u, 48 * u + 48), v("b1", 16 * u + 1, 1536, 32), v("ab", 48 * u, 48 * u + 48), A.mult)
-        scan(v("s4"), v("na"), v("ta"), 0.0, A.mult, A.add)
+                tt(v("g0", 96 * u + 1, 96 * u + 96, 2), v("b1", 16 * u, 1536, 32), v("m4", 48 * u, 48 * u + 48), A.is_le)
+            scan(v("g2"), v("g0"), v("g1"), 0.0, A.mult, A.add)
+            for h in range(2):
+                act(v("rin", 768 * h + 2, 768 * h + 768, 16), v("capr"), F.Identity, 0.0, bias=col(GID + h))
         for u in range(2):
-            copy(v("aoff", u, 24, 2), v("s4", 48 * u + 3, 48 * u + 48, 4))
+            copy(v("aoff", u, 24, 2), v("s4", 48 * u + 3, 48 * u + 48, 4) if t else v("g2", 96 * u + 7, 96 * u + 96, 8))
         for c in range(2):
-            off = v("aoff", 12 * c, 12 * c + 12)
             for b in range(2):
-                act(v("pb", C * b + H * c, C * b + H * c + H), (v("bh", B * (b + 2), B * (b + 3)), off))
-        if t == R - 1:
-            act(v("oar"), (v("jrow"), v("aoff")))
-            dma("Y", T.oa[:], T.oar[0:128:16, :], [v("oar")], [])
-        for c in range(2):
-            off = v("aoff", 12 * c, 12 * c + 12)
-            for b in range(2):
-                tt(v("yt", 4 * H * c + b, 4 * H * (c + 1), 4), (v("bh", B * b, B * b + B), off), v("fh", C * b + H * c, C * b + H * c + H), A.add)
-            for b in range(2):
-                tt(v("yt", 4 * H * c + b + 2, 4 * H * (c + 1), 4), v("pb", C * b + H * c, C * b + H * c + H), v("p%d" % (6 + b), H * c, H * c + H), A.add)
+                act(v("pb", C * b + H * c, C * b + H * c + H), (v("bh", B * (b + 2), B * (b + 3)), v("aoff", 12 * c, 12 * c + 12)))
+        qn, sn = "qt%d" % (t + 1), "st%d" % (t + 1)
+
+        def mean(c, b):
+            o = v("yt", 4 * H * c + b, 4 * H * (c + 1), 4)
+            if b < 2:
+                tt(o, (v("bh", B * b, B * b + B), v("aoff", 12 * c, 12 * c + 12)), v("fh", C * b + H * c, C * b + H * c + H), A.add)
+            else:
+                tt(o, v("pb", C * (b - 2) + H * c, C * (b - 2) + H * c + H), v("p%d" % (4 + b), H * c, H * c + H), A.add)
+
+        def layer(c):
             quant("qy", "sy", H * c, H * c + H, v("yt", 4 * H * c, 4 * H * (c + 1)))
             for b in range(4):
-                mx(4 + b % 2, "qw", "sw", 128 * b, "qy", "sy", H * c, H * c + H)
-                act(v("rr", C * b + H * c, C * b + H * c + H), v("p%d" % (4 + b % 2), 0, H), F.Relu, 2.0 ** -5)
-        qn, sn = "qt%d" % (t + 1), "st%d" % (t + 1)
-        for c in range(2):
-            for b in range(4):
-                tt(v("xt", 4 * H * c + b, 4 * H * (c + 1), 4), v("rr", C * b + H * c, C * b + H * c + H), v("p%d" % b, H * c, H * c + H), A.add)
+                k = 4 + (b if c else b % 2)
+                mx(k, "qw", "sw", 128 * b, "qy", "sy", H * c, H * c + H)
+                act(v("rr", C * b + H * c, C * b + H * c + H), v("p%d" % k, 0, H), F.Relu, 2.0 ** -5)
+
+        def state(c, b):
+            tt(v("xt", 4 * H * c + b, 4 * H * (c + 1), 4), v("rr", C * b + H * c, C * b + H * c + H), v("p%d" % b, H * c, H * c + H), A.add)
+
+        def close(c):
             quant(qn, sn, H * c, H * c + H, v("xt", 4 * H * c, 4 * H * (c + 1)))
             if t < R - 1:
                 scores(t + 1, c)
-                if c == 1 and t == EARLY - 1:
-                    copy(v("i2"), v("loff"))
-                    ts(col(U32), col(U), float(L), A.mult)
-                    ts(col(N32), col(U), -float(L), A.mult, float(L), A.add)
-                    ts(v("i3"), v("i2"), 15, A.bitwise_and)
-                    ts(v("f1"), v("i2"), 768.0, A.is_ge, 16.0, A.mult)
-                    tt(v("f2"), v("f1"), v("i3"), A.add)
-                    ts(v("goff", 0, 96, 2), v("f2", 0, 96, 2), col(U32), A.add)
-                    ts(v("goff", 1, 96, 2), v("f2", 1, 96, 2), col(N32), A.add)
-                if c == 1 and t == 1:
-                    quant("qv", "sv", 0, 128, v("vt"))
-            else:
-                mx(4 + c, "qv", "sv", 0, qn, sn, H * c, H * c + H)
-                dma("Y", T.oc[:, 4 * H * c:4 * H * (c + 1)], ap(v(qn, H * c, H * c + H)).bitcast(dt.uint8), [v(qn, H * c, H * c + H)], [])
-                act(v("yo", H * c, H * c + H), v("p%d" % (4 + c), 0, H))
-                dma("A", T.y[:, H * c:H * c + H], ap(v("yo", H * c, H * c + H)), [v("yo", H * c, H * c + H)], [])
-    for k in range(4):
-        dma("Y", T.osc[4 * k:4 * k + 4, :], T["st%d" % R][32 * k:32 * k + 4, 0:C], [v("st%d" % R, 0, C)], [])
+                return
+            mx(4 + c, "qv", "sv", 0, qn, sn, H * c, H * c + H)
+            dma("Y", T.oc[:, 4 * H * c:4 * H * (c + 1)], ap(v(qn, H * c, H * c + H)).bitcast(dt.uint8), [v(qn, H * c, H * c + H)], [])
+            for k in range(4 * c):
+                dma("YA"[k // 2], T.osc[4 * k:4 * k + 4, :], T[sn][32 * k:32 * k + 4, 0:C], [v(sn, 0, C)], [])
+            (copy if c else act)(v("yo", H * c, H * c + H), v("p%d" % (4 + c), 0, H))
+            dma("A", T.y[:, H * c:H * c + H], ap(v("yo", H * c, H * c + H)), [v("yo", H * c, H * c + H)], [])
+
+        for b in range(4):
+            mean(0, b)
+        layer(0)
+        if t == R - 1:
+            act(v("oar"), (v("jrow"), v("aoff")))
+            dma("Y", T.oa[:], T.oar[0:128:16, :], [v("oar")], [])
+        for b in range(4):
+            mean(1, b)
+        state(0, 0)
+        layer(1)
+        for b in range(1, 4):
+            state(0, b)
+        close(0)
+        for b in range(4):
+            state(1, b)
+        close(1)
     _emit(g, T, ops)
     g.wait_ge(T.sem.sent, sum(len(topo.engines(core, T.cores[(rank + 1 + t) % N])) // 2 * 2 for t in range(R)))

from concourse.bass import DstId, RemoteDMATransfer
from concourse.mybir import dt, AluOpType, ActivationFunctionType

C, L, S, R = 384, 32, 24, 3
H = C // 2
B = C + L
BIG = 1e29
CODE = "float8_e4m3fn_x4"
CUTS = (0, 224, 416, 768, 1088, 1344, 1536)


def _sb(n, d="float32"):
    return ("sbuf", [128, n], d)


SCRATCH = {
    "xt": _sb(4 * C, "bfloat16"), "yt": _sb(4 * C, "bfloat16"), "et": _sb(512, "bfloat16"),
    "ut": _sb(512, "bfloat16"), "vt": _sb(512, "bfloat16"), "bh": _sb(4 * B, "bfloat16"), "pb": _sb(2 * C, "bfloat16"),
    "fh": _sb(2 * C, "bfloat16"), "jb": _sb(12),
    "ones": _sb(516, "bfloat16"), "ida": _sb(516, "bfloat16"), "idb": _sb(516, "bfloat16"), "idh": _sb(1024, "bfloat16"),
    "cap16": _sb(C, "bfloat16"),
    "qu": _sb(128, CODE), "su": _sb(128, "uint8"), "qp": _sb(128, CODE), "sp": _sb(128, "uint8"),
    "qv": _sb(128, CODE), "sv": _sb(128, "uint8"), "qw": _sb(512, CODE), "sw": _sb(512, "uint8"),
    "qi": _sb(768, CODE), "si": _sb(768, "uint8"), "qy": _sb(C, CODE), "sy": _sb(C, "uint8"),
    "rti": _sb(48, "int32"), "fti": _sb(24, "int32"), "rowi": _sb(768, "int32"),
    "ci": _sb(8, "int32"), "cf": _sb(16), "i1": _sb(144), "i2": _sb(96, "int32"), "i3": _sb(96, "int32"),
    "i4": _sb(96, "int32"), "iu": _sb(8, "int32"), "fld": _sb(576, "int32"), "eq": _sb(16), "i16": _sb(16),
    "capr": _sb(48), "cap4": _sb(96), "jrow": _sb(B), "tab": _sb(576), "key": _sb(96), "sums": _sb(12),
    "uoff": _sb(8, "uint16"), "koff": _sb(96, "uint16"), "zoff": _sb(48, "uint16"), "roff": _sb(48, "uint16"),
    "foff": _sb(24, "uint16"), "coff": _sb(48, "uint16"), "loff": _sb(96, "uint16"), "eoff": _sb(8, "uint16"),
    "aoff": _sb(24, "uint16"), "goff": _sb(96, "uint16"), "gwin": _sb(2 * L), "vv": _sb(96),
    "way": _sb(48), "wrow": _sb(768), "swin": _sb(768), "b0": _sb(1536), "b1": _sb(1536), "b2": _sb(1536), "b3": _sb(1536),
    "rin": _sb(1536), "rr": _sb(4 * C), "mm": _sb(49), "ss": _sb(98), "na": _sb(96),
    "w0": _sb(96), "w1": _sb(96), "g0": _sb(192), "g1": _sb(192), "g2": _sb(192),
    "md": _sb(96), "sd": _sb(96), "gg": _sb(64), "q4": _sb(4), "tp": _sb(96), "m4": _sb(97), "s4": _sb(96),
    "e0": _sb(288), "e1": _sb(288), "e2": _sb(288),
    "f1": _sb(96), "f2": _sb(96), "yo": _sb(C), "oar": _sb(C),
}
for _t in range(R + 1):
    SCRATCH["qt%d" % _t] = _sb(B, CODE)
    SCRATCH["st%d" % _t] = _sb(512, "uint8")
for _t in range(R):
    SCRATCH["qe%d" % _t] = _sb(128, CODE)
    SCRATCH["se%d" % _t] = _sb(128, "uint8")
for _b in range(8):
    SCRATCH["p%d" % _b] = ("psum", [128, 512], "float32")

SEMAPHORES = ["sent", "v", "a", "p", "g"] + ["arr%d" % t for t in range(R)] + ["d%d" % i for i in range(24)]


def _mask(v):
    m = 0
    for j in range(v[1], v[2], v[3]):
        m |= 1 << j
    return m


def _emit(g, T, ops):
    queue = {"V": g.vector, "A": g.scalar, "P": g.tensor, "G": g, "Y": g.sync}
    seen = {}
    for n, o in enumerate(ops):
        deps = set()
        for v, wr in [(v, False) for v in o["r"]] + [(v, True) for v in o["w"]]:
            m = _mask(v)
            psum = SCRATCH[v[0]][0] == "psum"
            for e in seen.setdefault(v[0], []):
                if (e[1] & m and (wr or e[2])) or (psum and ops[e[0]]["q"] != o["q"]):
                    deps.add(e[0])
        for v, wr in [(v, False) for v in o["r"]] + [(v, True) for v in o["w"]]:
            m = _mask(v)
            lst = seen[v[0]]
            if wr:
                for e in lst:
                    e[1] &= ~m
                lst[:] = [e for e in lst if e[1]]
            lst.append([n, m, wr])
        deps.discard(n)
        o["deps"] = deps
    known = {q: set() for q in queue}
    earlier = {q: [] for q in queue}
    for n, o in enumerate(ops):
        o["waits"] = []
        if o["q"] is None:
            o["known"] = set()
            continue
        k = known[o["q"]]
        for d in sorted(o["deps"], reverse=True):
            if d not in k:
                o["waits"].append(d)
                ops[d]["needed"] = True
                k.add(d)
                k |= ops[d]["known"]
        o["known"] = set(k)
        if not o["dma"]:
            o["known"] |= set(earlier[o["q"]])
            earlier[o["q"]].append(n)
    count, dmas, last = {}, 0, []
    for o in ops:
        if o["q"] is None:
            continue
        q = queue[o["q"]]
        for d in o["waits"]:
            q.wait_ge(T.sem[ops[d]["sig"][0]], ops[d]["sig"][1])
        ins = o["f"]()
        if o["dma"]:
            o["sig"] = ("d%d" % dmas, 16)
            dmas += 1
            ins.then_inc(T.sem[o["sig"][0]], 16)
            if not o.get("needed"):
                last.append((q, o["sig"]))
        elif o.get("needed"):
            name = o["q"].lower()
            count[name] = count.get(name, 0) + 1
            o["sig"] = (name, count[name])
            ins.then_inc(T.sem[name], 1)
    for q, sig in last:
        q.wait_ge(T.sem[sig[0]], sig[1])


def rank_program(g, core, T, topo):
    rank = T.rank_of(core)
    if rank is None:
        return
    N = len(T.cores)
    A, F = AluOpType, ActivationFunctionType
    ops = []

    def v(name, a=0, b=None, s=1):
        return (name, a, SCRATCH[name][1][1] if b is None else b, s)

    def ap(x):
        if len(x) == 2:
            return ap(x[0]).indirect(ap(x[1]))
        return T[x[0]][:, x[1]:x[2]:x[3]] if x[3] != 1 else T[x[0]][:, x[1]:x[2]]

    def rd(*xs):
        out = []
        for x in xs:
            if isinstance(x, tuple):
                out += list(x) if len(x) == 2 else [x]
        return out

    def add(q, f, r, w, dma=False):
        ops.append({"q": q, "f": f, "r": r, "w": w, "dma": dma})

    def sc(x):
        return ap(x) if isinstance(x, tuple) else x

    def copy(o, i):
        add("V", lambda: g.vector.tensor_copy(ap(o), ap(i)), rd(i), [o])

    def tt(o, a, b, op):
        add("V", lambda: g.vector.tensor_tensor(ap(o), ap(a), ap(b), op), rd(a, b), [o])

    def ts(o, a, s1, op0, s2=None, op1=None):
        if op1 is None:
            add("V", lambda: g.vector.tensor_scalar(ap(o), ap(a), sc(s1), None, op0), rd(a, s1), [o])
        else:
            add("V", lambda: g.vector.tensor_scalar(ap(o), ap(a), sc(s1), sc(s2), op0, op1), rd(a, s1, s2), [o])

    def scan(o, a, b, init, op0, op1):
        add("V", lambda: g.vector.tensor_tensor_scan(ap(o), ap(a), ap(b), init, op0, op1), rd(a, b), [o])

    def fill(o, c):
        add("V", lambda: g.vector.memset(ap(o), c), [], [o])

    def turn(o, i):
        add("V", lambda: g.vector.transpose(ap(o), ap(i)), [i], [o])

    def act(o, i, func=F.Copy, scale=1.0, acc=None, bias=None):
        if bias is not None:
            add("A", lambda: g.scalar.activation(ap(o), ap(i), func, bias=ap(bias), scale=scale), rd(i, bias), [o])
        elif SCRATCH[o[0]][2] == "uint8":
            add("A", lambda: g.scalar.activation(ap(o), ap(i), func), rd(i), [o])
        elif acc is None:
            add("A", lambda: g.scalar.activation(ap(o), ap(i), func, scale=scale), rd(i), [o])
        else:
            add("A", lambda: g.scalar.activation(ap(o), ap(i), func, accum_out=ap(acc)), rd(i), [o, acc])

    def other(o, i):
        act(o, i, F.Identity, -1.0, bias=v("ones", 0, 1))

    def const(o, c):
        act(o, v("ones", 0, len(range(*o[1:]))), scale=c)

    def quant(q, s, a, b, i):
        add("V", lambda: g.vector.quantize_mx(ap(v(q, a, b)), ap(v(s, a, b)), ap(i)), [i], [v(q, a, b), v(s, a, b)])

    def mx(bank, lq, ls, la, rq, rs, a, b):
        x = [v(lq, la, la + 128), v(ls, la, la + 128), v(rq, a, b), v(rs, a, b)]
        o = v("p%d" % bank, 0, b - a)
        add("P", lambda: g.tensor.matmul_mx(ap(o), ap(x[0]), ap(x[1]), ap(x[2]), ap(x[3]), True, True), x, [o])

    def iota(o, pattern, base=0, cm=0):
        if SCRATCH[o[0]][2] == "int32":
            add("G", lambda: g.iota(ap(o), pattern, base, cm), [], [o])
        else:
            add("G", lambda: g.iota(ap(o), pattern, base, cm, allow_small_or_imprecise_dtypes=True), [], [o])

    def dma(q, out, in_, r, w):
        eng = g.sync if q == "Y" else g.scalar
        add(q, lambda: eng.dma_start(out, in_), r, w, True)

    def col(j):
        return v("cf", j, j + 1)

    K, U, K24, K16, GID, U384, N384, C32, U32, N32 = 0, 1, 2, 3, 4, 6, 7, 8, 9, 10

    fill(v("rowi"), 0)
    dma("Y", T.rti[:], T.rt[:], [], [v("rti")])
    dma("A", T.ut[:], T.u[:], [], [v("ut")])
    dma("Y", T.rowi[0:128:16, :], T.rt[:], [], [v("rowi")])
    for c in range(2):
        dma("Y", ap(v("xt", 4 * H * c, 4 * H * (c + 1))), T.x[:, 4 * H * c:4 * H * (c + 1)], [], [v("xt", 4 * H * c, 4 * H * (c + 1))])
    iota(v("ci", 0, 1), [[0, 1]], 0, 1)
    iota(v("i1", 0, 48), [[384, 2], [1, 24]])
    iota(v("i16"), [[1, 16]])
    iota(v("iu"), [[32, 4], [-16, 2]], 16)
    iota(v("i1", 48, 96), [[1, 16], [256, 3]])
    iota(v("i1", 96, 144), [[16, 48]])
    iota(v("jb"), [[32, 12]])
    fill(v("ones"), 1.0)
    for name, base in (("ida", 2), ("idb", 3)):
        add("G", lambda name=name, base=base: g.affine_select(T[name][:], T.ones[:], [[-1, 516]], A.is_equal, 0.0, base, 4),
            [v("ones")], [v(name)])
    iota(v("et", 4 * L, 512), [[0, 512 - 4 * L]])
    iota(v("jrow"), [[1, B]])
    ts(v("ci", 2, 3), v("ci", 0, 1), 15, A.bitwise_and)
    ts(v("ci", 3, 4), v("ci", 0, 1), 4, A.logical_shift_right, 1, A.bitwise_and)
    const(v("tab", 0, H), 0.0)
    const(v("tab", C, C + H), 0.0)
    copy(v("cf", 0, 2), v("ci", 2, 4))
    ts(col(K24), col(K), 24.0, A.mult)
    ts(v("eq"), v("i16"), col(K), A.is_equal)
    ts(col(K16), col(K), 16.0, A.mult)
    ts(v("i2", 0, 48), v("i1", 0, 48), col(K24), A.add)
    ts(col(U384), col(U), float(C), A.mult)
    ts(col(N384), col(U), -float(C), A.mult, float(C), A.add)
    ts(v("i3", 0, 48), v("i2", 0, 48), 15, A.bitwise_and)
    ts(v("i4", 0, 48), v("i2", 0, 48), 4, A.logical_shift_right)
    for m in range(12):
        act(v("tab", H + 16 * m, H + 16 * m + 16), v("eq"), scale=4.0 ** (3 * (m % 4) + m // 4))
    const(v("capr"), BIG)
    for b in range(4):
        const(v("q4", b, b + 1), b / 4)
    const(v("mm", 0, 1), -BIG)
    const(v("m4", 0, 1), -BIG)
    const(v("ss", 1, 2), 0.0)
    const(v("w0", 0, 96, 2), 1.0)
    const(v("capr", S - 1, 48, S), -BIG)
    ts(col(GID), col(K), float(C), A.add)
    ts(v("i3", 0, 48), v("i3", 0, 48), 48.0, A.mult)
    ts(col(GID + 1), col(K), float(C + 16), A.add)
    ts(col(C32), col(U), 16.0, A.mult, col(K), A.add)
    tt(v("i2", 0, 48), v("i3", 0, 48), v("i4", 0, 48), A.add)
    copy(v("uoff"), v("iu"))
    ts(v("koff", 48, 96), v("i1", 48, 96), col(K16), A.add)
    copy(v("koff", 0, 48), v("i2", 0, 48))
    copy(v("roff"), v("rti"))
    ts(col(U32), col(U), float(L), A.mult)
    ts(col(N32), col(U), -float(L), A.mult, float(L), A.add)
    ts(v("f2", 0, 48), v("i1", 96, 144), col(K), A.add)
    ts(v("jb"), v("jb"), col(C32), A.add, -2048.0, A.mult)
    quant("qu", "su", 0, 128, v("ut"))

    def counts(p):
        act(v("b2", 768 * p, 768 * p + 768), (v("tab", H * (1 - p), H * (1 - p) + C), v("roff")))

    def running(p):
        x = v("b2", 768 * p, 768 * p + 768)
        scan(v("rin", 768 * p, 768 * p + 768), x, x, 0.0, A.add, A.max)

    copy(v("b0", 0, 768), (v("rowi"), v("koff", 0, 48)))
    counts(0)
    add("V", lambda: g.vector.tensor_copy(T.qp[:, 0:128].bitcast(dt.uint32), T.qu[:, 0:128].bitcast(dt.uint32).indirect(T.uoff[:, 0:8])),
        [v("qu"), v("uoff")], [v("qp")])
    act(v("sp"), (v("su"), v("uoff")))
    act(v("wrow"), (v("b0", 0, 768), v("koff", 48, 96)))
    dma("Y", T.way[:], T.wrow[0:128:16, :], [v("wrow")], [v("way")])
    dma("Y", T.fti[:], T.ft[:], [], [v("fti")])
    dma("Y", T.qw[:].bitcast(dt.uint8), T.wc[:], [v("way")], [v("qw")])
    dma("Y", T.sw[:], T.ws[:], [], [v("sw")])
    dma("Y", T.vt[:], T.v[:], [], [v("vt")])

    def scores(t, c):
        mx(4 + 2 * c, "qu", "su", 0, "qt%d" % t, "st%d" % t, H * c, H * c + H)
        mx(5 + 2 * c, "qp", "sp", 0, "qt%d" % t, "st%d" % t, H * c, H * c + H)
        act(v("swin", H * c, H * c + H), v("p%d" % (4 + 2 * c), 0, H))
        (act if c == 0 or t == 0 else copy)(v("swin", C + H * c, C + H * c + H), v("p%d" % (5 + 2 * c), 0, H))

    turn(v("b1", 0, 768), v("b0", 0, 768))
    for c in range(2):
        quant("qt0", "st0", H * c, H * c + H, v("xt", 4 * H * c, 4 * H * (c + 1)))
        scores(0, c)
    ts(v("zoff", 0, 48, 2), v("b1", 0, 768, 32), col(U384), A.add)
    ts(v("zoff", 1, 48, 2), v("b1", 16, 768, 32), col(N384), A.add)
    running(0)

    def places():
        running(1)
        for d in range(2):
            act(v("md", d, 96, 2), v("mm", 0, 48))
            act(v("sd", d, 96, 2), v("ss", 1, 97, 2))
        const(v("cap16"), -1.0)
        const(v("cap4"), BIG)
        for b in range(2):
            act(v("idh", 512 * b, 512 * b + 512), v("idb" if b else "ida", 0, 512), scale=0.5)
        const(v("cap16", 0, C, 16), 2.0 ** 21)
        const(v("cap4", 3, 96, 4), -BIG)
        tt(v("f1", 48, 96), v("f1", 0, 48), v("f2", 0, 48), A.subtract)
        tt(v("key", 0, 48), v("f1", 0, 48), v("f2", 0, 48), A.add)
        copy(v("i2"), v("rin", 15, 1536, 16))
        ts(v("key", 48, 96), v("f1", 48, 96), 1023.0, A.add)
        copy(v("foff"), v("fti"))
        for r in range(6):
            ts(v("fld", 96 * r, 96 * r + 96), v("i2"), r, A.logical_shift_right, 0x041041, A.bitwise_and)
        for h in range(2):
            copy(v("b0", 288 * h, 288 * h + 288), v("fld", 288 * h, 288 * h + 288))
            for r in range(3 * h, 3 * h + 3):
                for p in range(2):
                    j = 6 * (r % 2) + 3 * p + r // 2
                    act(v("b1", 48 * j, 48 * j + 48), v("b0", 96 * r + 48 * p, 96 * r + 48 * p + 48), acc=v("sums", j, j + 1))
        quant("qi", "si", 512, 768, v("idh"))
        ident(0, 2)
        ident(0, 3)
        copy(v("i3", 0, 12), v("sums"))
        for f in range(4):
            ts(v("i4", f, 48, 4), v("i3", 0, 12), 6 * f, A.logical_shift_right, 63, A.bitwise_and)
        tt(v("i4", 0, 24), v("i4", 0, 24), v("i4", 24, 48), A.add)
        for p in (1, 0):
            for h in range(2):
                ts(v("coff", 2 * p + h, 48, 4), v("i4", 24 * p + h, 24 * p + 24, 2), -1.0, A.mult, 48.0 * (p + 1), A.add)
        act(v("b0", C, 2 * C), (v("key"), v("coff", 24, 48)))
        copy(v("b0", 0, H), (v("key"), v("coff", 0, 12)))
        copy(v("b0", H, C), (v("key"), v("coff", 12, 24)))
        for j in range(4):
            turn(v("b1", H * j, H * j + H), v("b0", H * j, H * j + H))
        for b in range(12):
            act(v("b2", 64 * b, 64 * b + 64), v("b1", 64 * b, 64 * b + 64), F.Abs, bias=v("jb", b, b + 1))
        for j in range(4):
            scan(v("b3", H * j, H * j + H), v("cap16", 0, H), v("b2", H * j, H * j + H), 0.0, A.max, A.min)
        unpack(0)
        for h in range(2):
            copy(v("i2", h, 24, 2), v("b3", 15 + 16 * h, 2 * C, 64))
            ts(v("i2", 24 + h, 48, 2), v("b3", 47 + 16 * h, 2 * C, 64), -1.0, A.mult, 1023.0, A.add)
        ts(v("i3", 0, 48), v("i2", 0, 48), 2731.0, A.mult)
        for h in range(2):
            ts(v("f1", h, 48, 2), v("i2", h, 48, 2), 32.0, A.mult, 16.0 * h, A.add)
        ts(v("i4", 0, 48), v("i3", 0, 48), 16, A.logical_shift_right)
        ts(v("i4", 48, 96), v("i3", 0, 48), 20, A.logical_shift_right)
        ts(v("f2", 0, 48), v("i4", 0, 48), -767.0, A.mult)
        ts(v("f2", 48, 96), v("i4", 48, 96), 752.0, A.mult)
        tt(v("f1", 48, 96), v("f1", 0, 48), v("f2", 0, 48), A.add)
        for p in range(2):
            tt(v("b0", p, C, 16), v("f1", 48 + 24 * p, 72 + 24 * p), v("f2", 48 + 24 * p, 72 + 24 * p), A.add)
        turn(v("b1", 0, C), v("b0", 0, C))

    def ident(t, b):
        if t == 0:
            quant("qi", "si", 128 * b, 128 * b + 128, v("idb" if b % 2 else "ida", 2 - b // 2 * 2, 514 - b // 2 * 2))

    def unpack(t):
        for b in range(4):
            mx(b, "qi", "si", 128 * b, "qt%d" % t, "st%d" % t, 0, C)
            if b < 2:
                act(v("bh", B * b, B * b + C), v("p%d" % b, 0, C), scale=0.5)
                act(v("fh", C * b, C * b + C), v("p%d" % b, 0, C), scale=0.5)
        for b in range(2):
            mx(6 + b, "qi", "si", 512 + 128 * b, "qt%d" % t, "st%d" % t, 0, C)

    def rest():
        for b in range(2, 4):
            act(v("bh", B * b, B * b + C), v("p%d" % b, 0, C), scale=0.5)

    def carry(win, off, to, cuts=CUTS):
        for j in range(len(cuts) - 1):
            (act if j > 1 else copy)(v("b0", cuts[j], cuts[j + 1]), (win, v(off, cuts[j] // 16, cuts[j + 1] // 16)))
        for j in range(len(cuts) - 1):
            turn(v(to, cuts[j], cuts[j + 1]), v("b0", cuts[j], cuts[j + 1]))

    for t in range(R):
        qt, st, qe, se = "qt%d" % t, "st%d" % t, "qe%d" % t, "se%d" % t
        carry(v("swin"), "zoff", "b1", (0, 128, 256, 512, 768))
        z = v("b1", 0, 768, 16)
        if t == 0:
            act(v("w1", 0, 96, 2), v("way"), scale=-1.0)
            act(v("w1", 1, 96, 2), v("way"))
            counts(1)
        scan(v("mm", 1, 49), z, v("capr"), -BIG, A.max, A.min)
        ident(t, 0)
        tt(v("w0", 1, 96, 2), z, v("mm", 0, 48), A.is_le)
        ident(t, 1)
        for d in range(2 if t else 0):
            act(v("rin", 16 * d, 1536, 32), v("mm", 0, 48))
        scan(v("ss", 2, 98), v("w0"), v("w1"), 0.0, A.mult, A.add)
        if t == 0:
            ts(v("f1", 0, 48), v("rti"), 2048.0, A.mult)
        for h in range(2):
            ts(v("eoff", h, 8, 2), v("q4"), v("ss", 2 * S * (h + 1) + 1, 2 * S * (h + 1) + 2), A.add, 4.0, A.mult)
        for d in range(2 if t else 0):
            act(v("rin", 16 * d + 1, 1536, 32), v("ss", 1, 97, 2))
        for b in range(4):
            (act if b % 2 and t else copy)(v("et", b, 4 * L, 4), (v("xt"), v("eoff", 2 * b, 2 * b + 2)))
        quant(qe, se, 0, 128, v("et"))
        dst = T.cores[(rank + 1 + t) % N]
        rid, pid = topo.addr(dst)[:2]
        eng = topo.engines(core, dst)
        half = len(eng) // 2
        masks = [sum(1 << e for e in eng[:half]), sum(1 << e for e in eng[half:2 * half])]

        def send(qt=qt, st=st, qe=qe, se=se, rid=rid, pid=pid, masks=masks, t=t):
            to = [DstId(rid=rid, pnc=pid)]
            return g.remote_dma_fused([
                RemoteDMATransfer(dst_ids=to, dma_engine_mask=masks[0], remote_sem=T.sem["arr%d" % t],
                                  src=T[qe][:, 0:L].bitcast(dt.uint8), dst=T[qt][:, C:B].bitcast(dt.uint8)),
                RemoteDMATransfer(dst_ids=to, dma_engine_mask=masks[1], remote_sem=T.sem["arr%d" % t],
                                  src=T[se][:, 0:128], dst=T[st][:, C:C + 128])], local_sem=T.sem.sent)

        add("G", send, [v(qe), v(se)], [])
        src = T.cores[(rank - 1 - t) % N]
        ops.append({"q": None, "r": [], "w": [v(qt, C, B), v(st, C, C + 128)], "dma": False,
                    "sig": ("arr%d" % t, len(topo.engines(src, core)) // 2 * 2)})

        def guests():
            for b in range(4):
                mx(5 - b % 2, "qi", "si", 128 * b, qt, st, B - 128, B)
                act(v("bh", B * b + C, B * b + B), v("p%d" % (5 - b % 2), 128 - L, 128), scale=0.5)

        if t:
            turn(v("b2"), v("rin"))
            if t == 1:
                copy(v("i2"), v("loff"))
                quant("qv", "sv", 0, 128, v("vt"))
            unpack(t)
            carry(v("b2"), "loff", "b1")
            for u in range(2):
                act(v("e1", 144 * u + 1, 144 * u + 144, 3), v("b1", 16 * u + 1, 1536, 32))
            if t == 1:
                for u in range(2):
                    act(v("e1", 144 * u, 144 * u + 144, 3), v("b1", 16 * u + 2, 1536, 32))
                ts(v("f1"), v("i2"), 768.0, A.is_ge, 16.0, A.mult)
                ts(v("i3"), v("i2"), 15, A.bitwise_and)
                tt(v("f2"), v("f1"), v("i3"), A.add)
                ts(v("goff", 0, 96, 2), v("f2", 0, 96, 2), col(U32), A.add)
                ts(v("goff", 1, 96, 2), v("f2", 1, 96, 2), col(N32), A.add)
            mx(4, "qu", "su", 0, qt, st, B - 128, B)
            mx(5, "qp", "sp", 0, qt, st, B - 128, B)
            act(v("gwin", 0, L), v("p4", 128 - L, 128))
            copy(v("gwin", L, 2 * L), v("p5", 128 - L, 128))
            carry(v("gwin"), "goff", "b3")
            guests()
            rest()
            for u in range(2):
                tt(v("vv", 48 * u, 48 * u + 48), v("b1", 16 * u, 1536, 32), v("b3", 16 * u, 1536, 32), A.max)
            tt(v("e0", 1, 144, 3), v("b1", 0, 1536, 32), v("b3", 0, 1536, 32), A.is_le)
            scan(v("m4", 1, 97), v("vv"), v("cap4"), -BIG, A.max, A.min)
            tt(v("e0", 145, 288, 3), v("b1", 16, 1536, 32), v("b3", 16, 1536, 32), A.is_le)
            tt(v("e0", 2, 288, 3), v("vv"), v("m4", 0, 96), A.is_gt)
            other(v("na"), v("e0", 2, 288, 3))
            scan(v("e2"), v("e0"), v("e1"), 0.0, A.mult, A.max)
            scan(v("s4"), v("na"), v("e2", 2, 288, 3), 0.0, A.mult, A.add)
        else:
            places()
            mx(4, "qu", "su", 0, qt, st, B - 128, B)
            mx(5, "qp", "sp", 0, qt, st, B - 128, B)
            act(v("wrow", 0, C), (v("b1", 0, C), v("foff")))
            for p in range(2):
                for h in range(2):
                    copy(v("loff", 2 * p + h, 96, 8), v("b0", 16 * h + p, C, 32))
            for h in range(2):
                copy(v("gwin", 32 * h, 32 * h + 16), v("p4", 96 + 16 * h, 112 + 16 * h))
            for h in range(2):
                copy(v("gwin", 32 * h + 16, 32 * h + 32), v("p5", 96 + 16 * h, 112 + 16 * h))
            turn(v("b3", 0, C), v("wrow", 0, C))
            turn(v("gg"), v("gwin"))
            guests()
            for p in range(2):
                for h in range(2):
                    copy(v("loff", 4 + 2 * p + h, 96, 8), v("b3", 16 * h + p, C, 32))
            for h in range(2):
                ts(v("tp", 48 * h, 48 * h + 48), v("md", 48 * h, 48 * h + 48), v("gg", 32 * h, 32 * h + 1), A.is_le, col(GID + h), A.mult)
            for h in range(2):
                ts(v("rin", 768 * h, 768 * h + 768, 16), v("md", 48 * h, 48 * h + 48), v("gg", 32 * h, 32 * h + 1), A.max)
            tt(v("rin", 1, 1536, 16), v("tp"), v("sd"), A.max)
            turn(v("b2"), v("rin"))
            const(v("e0", 0, 288, 3), 0.0)
            const(v("e1", 2, 288, 3), 0.0)
            const(v("g0", 0, 192, 2), 1.0)
            rest()
            carry(v("b2"), "loff", "b1")
            for u in range(2):
                scan(v("m4", 1 + 48 * u, 49 + 48 * u), v("b1", 16 * u, 1536, 32), v("cap4", 0, 48), -BIG, A.max, A.min)
            for u in range(2):
                act(v("g1", 96 * u, 96 * u + 96, 2), v("b1", 16 * u + 1, 1536, 32), scale=-1.0)
                act(v("g1", 96 * u + 1, 96 * u + 96, 2), v("b1", 16 * u + 1, 1536, 32))
            for u in range(2):
                tt(v("g0", 96 * u + 1, 96 * u + 96, 2), v("b1", 16 * u, 1536, 32), v("m4", 48 * u, 48 * u + 48), A.is_le)
            scan(v("g2"), v("g0"), v("g1"), 0.0, A.mult, A.add)
            for h in range(2):
                act(v("rin", 768 * h + 2, 768 * h + 768, 16), v("capr"), F.Identity, 0.0, bias=col(GID + h))
        for u in range(2):
            copy(v("aoff", u, 24, 2), v("s4", 48 * u + 3, 48 * u + 48, 4) if t else v("g2", 96 * u + 7, 96 * u + 96, 8))
        for c in range(2):
            for b in range(2):
                act(v("pb", C * b + H * c, C * b + H * c + H), (v("bh", B * (b + 2), B * (b + 3)), v("aoff", 12 * c, 12 * c + 12)))
        qn, sn = "qt%d" % (t + 1), "st%d" % (t + 1)

        def mean(c, b):
            o = v("yt", 4 * H * c + b, 4 * H * (c + 1), 4)
            if b < 2:
                tt(o, (v("bh", B * b, B * b + B), v("aoff", 12 * c, 12 * c + 12)), v("fh", C * b + H * c, C * b + H * c + H), A.add)
            else:
                tt(o, v("pb", C * (b - 2) + H * c, C * (b - 2) + H * c + H), v("p%d" % (4 + b), H * c, H * c + H), A.add)

        def layer(c):
            quant("qy", "sy", H * c, H * c + H, v("yt", 4 * H * c, 4 * H * (c + 1)))
            for b in range(4):
                k = 4 + (b if c else b % 2)
                mx(k, "qw", "sw", 128 * b, "qy", "sy", H * c, H * c + H)
                act(v("rr", C * b + H * c, C * b + H * c + H), v("p%d" % k, 0, H), F.Relu, 2.0 ** -5)

        def state(c, b):
            tt(v("xt", 4 * H * c + b, 4 * H * (c + 1), 4), v("rr", C * b + H * c, C * b + H * c + H), v("p%d" % b, H * c, H * c + H), A.add)

        def close(c):
            quant(qn, sn, H * c, H * c + H, v("xt", 4 * H * c, 4 * H * (c + 1)))
            if t < R - 1:
                scores(t + 1, c)
                return
            mx(4 + c, "qv", "sv", 0, qn, sn, H * c, H * c + H)
            dma("Y", T.oc[:, 4 * H * c:4 * H * (c + 1)], ap(v(qn, H * c, H * c + H)).bitcast(dt.uint8), [v(qn, H * c, H * c + H)], [])
            for k in range(4 * c):
                dma("YA"[k // 2], T.osc[4 * k:4 * k + 4, :], T[sn][32 * k:32 * k + 4, 0:C], [v(sn, 0, C)], [])
            (copy if c else act)(v("yo", H * c, H * c + H), v("p%d" % (4 + c), 0, H))
            dma("A", T.y[:, H * c:H * c + H], ap(v("yo", H * c, H * c + H)), [v("yo", H * c, H * c + H)], [])

        for b in range(4):
            mean(0, b)
        layer(0)
        if t == R - 1:
            act(v("oar"), (v("jrow"), v("aoff")))
            dma("Y", T.oa[:], T.oar[0:128:16, :], [v("oar")], [])
        for b in range(4):
            mean(1, b)
        state(0, 0)
        layer(1)
        for b in range(1, 4):
            state(0, b)
        close(0)
        for b in range(4):
            state(1, b)
        close(1)
    _emit(g, T, ops)
    g.wait_ge(T.sem.sent, sum(len(topo.engines(core, T.cores[(rank + 1 + t) % N])) // 2 * 2 for t in range(R)))
